import numpy as np
import ml_dtypes


def mxq(x, axis, fmt="e4m3"):
    dtype, down = {"e4m3": (ml_dtypes.float8_e4m3fn, 7), "e5m2": (ml_dtypes.float8_e5m2, 14)}[fmt]
    v = np.moveaxis(np.asarray(x, np.float32).astype(ml_dtypes.bfloat16).astype(np.float64), axis, -1)
    blocks = v.reshape(v.shape[:-1] + (-1, 32))
    amax = np.abs(blocks).max(-1, keepdims=True)
    byte = np.maximum(np.where(amax > 0, np.frexp(amax)[1] - 1 + 127, 0) - down, 1)
    scale = np.exp2(byte - 127.0)
    codes = (blocks / scale).astype(np.float32).astype(dtype).astype(np.float64)
    return np.moveaxis((codes * scale).reshape(v.shape), -1, axis)


WIDE = False


def mx_kscale(k):
    if not WIDE:
        return np.ones(k)
    levels = np.array([10, -10, 5, -5, 0])
    if k % 512:
        return np.exp2(np.random.permutation(np.resize(levels, k // 32))).repeat(32)
    a = np.empty((k // 512, 16))
    for p in range(k // 512):
        a[p, :8] = np.random.permutation(np.resize(levels, 8))
        for g in range(8):
            far = levels[np.abs(levels - a[p, g]) >= 10]
            a[p, g + 8] = far[np.random.randint(len(far))]
    return np.exp2(a.ravel()).repeat(32)


def f64(x):
    return np.asarray(x).astype(np.float64)


def striped(idx):
    return np.tile(idx.reshape(-1, 16).T, (8, 1)).astype(np.uint16)


def unstriped(offs):
    return offs[:16].T.reshape(-1).astype(np.int64)


def pack_weight(w):
    k, n = w.shape
    w = f64(np.asarray(w, np.float32).astype(ml_dtypes.bfloat16)).reshape(k // 32, 32, n)
    amax = np.abs(w).max(1)
    byte = np.clip(np.where(amax > 0, np.frexp(amax)[1] - 1 + 127 - 7, 1), 1, 254)
    scaled = (w * np.exp2(127.0 - byte)[:, None, :]).reshape(k, n).astype(np.float32)
    words = np.ascontiguousarray(scaled.reshape(k // 512, 128, 4, n).transpose(0, 1, 3, 2)).astype(ml_dtypes.float8_e4m3fn).view(np.uint8)
    return words, np.ascontiguousarray(byte.astype(np.uint8).reshape(k // 512, 16, n))


def unpack_weight(words, scales):
    g, p, n, _ = words.shape
    vals = np.ascontiguousarray(words).view(ml_dtypes.float8_e4m3fn).astype(np.float64) * np.repeat(np.exp2(scales.astype(np.float64) - 127.0), 8, axis=1)[..., None]
    return vals.transpose(0, 1, 3, 2).reshape(g * 512, n)


K, T, S, H, V, W = 512, 1024, 512, 512, 512, 2048
P = 2 ** 7


def setup_inputs():
    n = np.random.standard_normal
    s = mx_kscale(K)[:, None]
    u = mx_kscale(H)
    packed_xT = pack_weight(n((K, T)) * s)
    packed_eT = pack_weight(n((H, W)) / np.sqrt(H) / u[:, None])
    return {
        "x_words": packed_xT[0],
        "x_scales": packed_xT[1],
        "w1": (n((K, H)) / np.sqrt(K) / s * u).astype(np.float32),
        "e_words": packed_eT[0],
        "e_scales": packed_eT[1],
        "inv": (np.tile(np.random.uniform(0.5, 2.0, W), (P, 1))).astype(np.float32),
        "offs": striped(np.random.permutation(T)[:S]),
        "pro": striped(np.random.permutation(W)[:V]),
    }


def reference(x_words, x_scales, w1, e_words, e_scales, inv, offs, pro):
    xq = unpack_weight(x_words, x_scales)[:, unstriped(offs)]
    h = mxq(f64(w1), 0, "e4m3").T @ xq
    e_pro = unpack_weight(e_words, e_scales)[:, unstriped(pro)]
    y = mxq(h, 0, "e4m3").T @ e_pro
    z = y * (f64(inv)[:1][:, unstriped(pro)])
    ee = np.exp(z)
    l = np.log(ee.sum(axis=1, keepdims=True))
    return z - l

@@ -1,0 +1,152 @@
+import math
+from contextlib import ExitStack
+
+import concourse.mybir as mybir
+from concourse.masks import make_identity
+
+F32 = mybir.dt.float32
+BF16 = mybir.dt.bfloat16
+I32 = mybir.dt.int32
+U32 = mybir.dt.uint32
+U16 = mybir.dt.uint16
+U8 = mybir.dt.uint8
+FP8X4 = mybir.dt.float8_e4m3fn_x4
+ACT = mybir.ActivationFunctionType
+ALU = mybir.AluOpType
+AXIS = mybir.AxisListType
+
+P = 128
+PACK = 4
+K, T, S, H, V, W = 512, 1024, 512, 512, 512, 2048
+BLOCKS = S // P
+LOG_STEP = 0.375
+LOG_BELOW = 80
+LOG_ABOVE = 8
+INV_SPLIT = 1152
+
+FLOPS = 2 * K * H * S + 2 * H * S * V
+BYTES = K * T + K * T // 32 + 4 * K * H + H * W + H * W // 32 + 4 * W + 2 * P * (S + V) // 16 + 4 * S * V
+
+
+def tile_picked_yphi_log_p_kernel(tc, x_words, x_scales, w1, e_words, e_scales, inv, offs, pro, out):
+    nc = tc.nc
+    nodes = LOG_BELOW + LOG_ABOVE + 1
+    at_one = sum(math.tanh(math.e ** (LOG_STEP * j)) for j in range(-LOG_BELOW, LOG_ABOVE + 1))
+    ones = round(at_one)
+    node_shift = math.e ** (LOG_STEP * (ones - at_one))
+
+    with ExitStack() as ctx:
+        keep = ctx.enter_context(tc.tile_pool(name="keep", bufs=1))
+        psum = ctx.enter_context(tc.psum_pool(name="psum", bufs=1))
+
+        offs_sb = keep.tile([P, S // 16], U16, name="offs_sb")
+        pro_sb = keep.tile([P, V // 16], U16, name="pro_sb")
+        xs = keep.tile([P, T], U8, name="xs", align_bytes=64)
+        es = keep.tile([P, W], U8, name="es", align_bytes=64)
+        step_a = keep.tile([P, nodes], F32, name="step_a", tag="bytes_a", align_bytes=64)
+        step_b = keep.tile([P, nodes], F32, name="step_b", tag="bytes_b", align_bytes=64)
+        start = keep.tile([P, 1], F32, name="start", tag="bytes_c", align_bytes=64)
+        steps = keep.tile([P, nodes], F32, name="steps", tag="bytes_d", align_bytes=64)
+        grid0 = keep.tile([P, nodes], F32, name="grid0")
+        grid = keep.tile([P, ones + nodes], F32, name="grid")
+
+        nc.gpsimd.memset(xs[:].bitcast(I32), 0)
+        nc.gpsimd.memset(step_a[:], LOG_STEP / 2)
+        nc.vector.memset(step_b[:], LOG_STEP / 2)
+        nc.vector.memset(start[:], -LOG_STEP * (LOG_BELOW + 1))
+        nc.vector.tensor_tensor_scan(steps[:], step_a[:], step_b[:], start[:], ALU.add, ALU.add)
+        inv_row = keep.tile([P, W], F32, name="inv_row", tag="bytes_c", align_bytes=64)
+        nc.vector.memset(inv_row[:, 0:INV_SPLIT], 0.0)
+        nc.gpsimd.memset(inv_row[:, INV_SPLIT:], 0.0)
+        nc.gpsimd.memset(es[:].bitcast(I32), 0)
+        nc.scalar.activation(grid0[:], steps[:], ACT.Exp)
+        nc.vector.memset(grid[:, 0:ones], -32.0)
+        nc.vector.tensor_scalar(grid[:, ones:], grid0[:], node_shift, None, ALU.mult)
+        ident = keep.tile([P, P], F32, name="ident", align_bytes=64)
+        make_identity(nc, ident[:])
+
+        w_raw = [keep.tile([P, PACK, H // 2], F32, name=f"w_raw{u}", tag=tag, align_bytes=64) for u, tag in enumerate(("bytes_a", "bytes_b"))]
+        xw = keep.tile([P, T], U32, name="xw", align_bytes=64)
+        ew = keep.tile([P, W], U32, name="ew", tag="bytes_d", align_bytes=64)
+        w_rows = w1.rearrange("(p j) c -> p j c", j=PACK)
+        nc.sync.dma_start(offs_sb[:], offs)
+        nc.sync.dma_start(pro_sb[:], pro)
+        nc.sync.dma_start(xw[:].bitcast(I32), x_words[0].rearrange("p n t -> p (n t)").bitcast(I32))
+        for q in range(4):
+            nc.scalar.dma_start(xs[32 * q : 32 * q + 4, :].bitcast(I32), x_scales[0, 4 * q : 4 * q + 4, :].bitcast(I32))
+        nc.sync.dma_start(w_raw[0][:], w_rows[:, :, 0 : H // 2])
+        nc.sync.dma_start(w_raw[1][:], w_rows[:, :, H // 2 : H])
+        nc.sync.dma_start(inv_row[0:1, :], inv[0:1, :])
+        for q in range(4):
+            nc.sync.dma_start(es[32 * q : 32 * q + 4, :].bitcast(I32), e_scales[0, 4 * q : 4 * q + 4, :].bitcast(I32))
+        nc.sync.dma_start(ew[:].bitcast(I32), e_words[0].rearrange("p n t -> p (n t)").bitcast(I32))
+
+        xsg = keep.tile([P, S], U8, name="xsg", align_bytes=64)
+        esg = keep.tile([P, V], U8, name="esg", align_bytes=64)
+        xwg = keep.tile([P, S], U32, name="xwg", align_bytes=64)
+        ewg = keep.tile([P, V], U32, name="ewg", align_bytes=64)
+        invg = keep.tile([P, V], F32, name="invg", align_bytes=64)
+        nc.vector.tensor_copy(xsg[:], xs[:].indirect(offs_sb[:]))
+        nc.vector.tensor_copy(xwg[:], xw[:].indirect(offs_sb[:]))
+        nc.vector.tensor_copy(invg[:], inv_row[:].indirect(pro_sb[:]))
+
+        wg = keep.tile([P, PACK, P, PACK], BF16, name="wg", align_bytes=64)
+        for u in range(2):
+            nc.scalar.copy(
+                wg[:, :, u * P // 2 : (u + 1) * P // 2, :].rearrange("p t m j -> p m t j"),
+                w_raw[u][:].rearrange("p j (m t) -> p m t j", t=PACK),
+            )
+        wc = keep.tile([P, H], U32, name="wc", align_bytes=64)
+        ws = keep.tile([P, H], U8, name="ws", align_bytes=64)
+        nc.vector.quantize_mx(out=wc[:].bitcast(FP8X4), scales=ws[:], in_=wg[:].rearrange("p t m j -> p (t m j)"))
+        nc.vector.tensor_copy(esg[:], es[:].indirect(pro_sb[:]))
+        nc.vector.tensor_copy(ewg[:], ew[:].indirect(pro_sb[:]))
+
+        turned = psum.tile([P, V // P, P], F32, name="turned")
+        for c in range(V // P):
+            nc.tensor.transpose(turned[:, c, :], invg[:, c * P : (c + 1) * P], ident[:])
+        inv_col = keep.tile([P, V // P], F32, name="inv_col", tag="bytes_b", align_bytes=64)
+        nc.scalar.copy(inv_col[:], turned[:, :, 0])
+        spread = psum.tile([P, V], F32, name="spread")
+        for c in range(V // P):
+            nc.tensor.transpose(spread[:, c * P : (c + 1) * P], inv_col[:, c : c + 1].to_broadcast([P, P]), ident[:])
+        inv_all = keep.tile([P, V], F32, name="inv_all", align_bytes=64)
+        nc.scalar.copy(inv_all[:], spread[:])
+
+        hc = keep.tile([P, S], U32, name="hc", align_bytes=64)
+        hs = keep.tile([P, S], U8, name="hs", tag="bytes_d", align_bytes=64)
+        for b in range(BLOCKS):
+            cols = slice(b * P, (b + 1) * P)
+            hp = psum.tile([P, PACK, P], F32, name=f"hp{b}", tag="hp", bufs=4)
+            for t in range(PACK):
+                tcols = slice(t * P, (t + 1) * P)
+                nc.tensor.matmul_mx(out=hp[:, t, :], lhsT=wc[:, tcols].bitcast(FP8X4), lhsT_scale=ws[:, tcols],
+                                    rhs=xwg[:, cols].bitcast(FP8X4), rhs_scale=xsg[:, cols], start=True, stop=True)
+            hb = keep.tile([P, P, PACK], BF16, name=f"hb{b}", align_bytes=64)
+            nc.scalar.copy(hb[:], hp[:].rearrange("p t n -> p n t"))
+            nc.vector.quantize_mx(out=hc[:, cols].bitcast(FP8X4), scales=hs[:, cols], in_=hb[:].rearrange("p n t -> p (n t)"))
+
+        junk = [keep.tile([P, V], F32, name=f"junk{u}", align_bytes=64) for u in range(2)]
+        for b in range(BLOCKS):
+            cols = slice(b * P, (b + 1) * P)
+            yp = psum.tile([P, V], F32, name=f"yp{b}", tag="yp", bufs=2)
+            nc.tensor.matmul_mx(out=yp[:], lhsT=hc[:, cols].bitcast(FP8X4), lhsT_scale=hs[:, cols],
+                                rhs=ewg[:].bitcast(FP8X4), rhs_scale=esg[:], start=True, stop=True)
+            z = keep.tile([P, V], F32, name=f"z{b}", align_bytes=64)
+            nc.vector.tensor_tensor(z[:], yp[:], inv_all[:], ALU.mult)
+            neg_max = keep.tile([P, 1], F32, name=f"neg_max{b}")
+            nc.vector.tensor_reduce(neg_max[:], z[:], AXIS.X, ALU.max, negate=True)
+            total = keep.tile([P, 1], F32, name=f"total{b}")
+            nc.scalar.activation(junk[b % 2][:], z[:], ACT.Exp, bias=neg_max[:], accum_out=total[:])
+            log_steps = keep.tile([P, 1], F32, name=f"log_steps{b}")
+            nc.scalar.activation(junk[b % 2][:, 0 : ones + nodes], grid[:], ACT.Tanh, scale=total[:], accum_out=log_steps[:])
+            res = keep.tile([P, V], F32, name=f"res{b}", align_bytes=64)
+            if b < BLOCKS - 2:
+                shift = keep.tile([P, 1], F32, name=f"shift{b}")
+                nc.gpsimd.tensor_scalar(shift[:], log_steps[:], -LOG_STEP, neg_max[:], ALU.mult, ALU.add)
+                nc.gpsimd.tensor_scalar(res[:], z[:], shift[:], 1.0, ALU.add, ALU.mult)
+            else:
+                centred = keep.tile([P, V], F32, name=f"centred{b}", align_bytes=64)
+                nc.vector.tensor_scalar(centred[:], z[:], neg_max[:], 1.0 / LOG_STEP, ALU.add, ALU.mult)
+                nc.vector.tensor_scalar(res[:], centred[:], log_steps[:], LOG_STEP, ALU.subtract, ALU.mult)
+            nc.sync.dma_start(out[cols, :], res[:])

@@ -89,6 +89,10 @@ def tile_picked_yphi_log_p_kernel(tc, x_words, x_scales, w1, e_words, e_scales, 
         nc.vector.tensor_copy(xsg[:], xs[:].indirect(offs_sb[:]))
         nc.vector.tensor_copy(xwg[:], xw[:].indirect(offs_sb[:]))
         nc.vector.tensor_copy(invg[:], inv_row[:].indirect(pro_sb[:]))
+        for u in range(2):
+            warm = psum.tile([P, S], F32, name=f"warm{u}", tag="yp", bufs=2)
+            nc.tensor.matmul_mx(out=warm[:], lhsT=xwg[:, 0:P].bitcast(FP8X4), lhsT_scale=xsg[:, 0:P],
+                                rhs=xwg[:].bitcast(FP8X4), rhs_scale=xsg[:], start=True, stop=True)
 
         wg = keep.tile([P, PACK, P, PACK], BF16, name="wg", align_bytes=64)
         for u in range(2):
@@ -143,7 +147,7 @@ def tile_picked_yphi_log_p_kernel(tc, x_words, x_scales, w1, e_words, e_scales, 
             res = keep.tile([P, V], F32, name=f"res{b}", align_bytes=64)
             if b < BLOCKS - 2:
                 shift = keep.tile([P, 1], F32, name=f"shift{b}")
-                nc.gpsimd.tensor_scalar(shift[:], log_steps[:], -LOG_STEP, neg_max[:], ALU.mult, ALU.add)
+                nc.scalar.activation(shift[:], log_steps[:], ACT.Identity, bias=neg_max[:], scale=-LOG_STEP)
                 nc.gpsimd.tensor_scalar(res[:], z[:], shift[:], 1.0, ALU.add, ALU.mult)
             else:
                 centred = keep.tile([P, V], F32, name=f"centred{b}", align_bytes=64)

@@ -22,7 +22,8 @@ BLOCKS = S // P
 LOG_STEP = 0.375
 LOG_BELOW = 80
 LOG_ABOVE = 8
-INV_SPLIT = 1152
+W_HALF_BYTES = PACK * (H // 2) * 4
+INV_SPLIT = 1408
 
 FLOPS = 2 * K * H * S + 2 * H * S * V
 BYTES = K * T + K * T // 32 + 4 * K * H + H * W + H * W // 32 + 4 * W + 2 * P * (S + V) // 16 + 4 * S * V
@@ -33,66 +34,62 @@ def tile_picked_yphi_log_p_kernel(tc, x_words, x_scales, w1, e_words, e_scales, 
     nodes = LOG_BELOW + LOG_ABOVE + 1
     at_one = sum(math.tanh(math.e ** (LOG_STEP * j)) for j in range(-LOG_BELOW, LOG_ABOVE + 1))
     ones = round(at_one)
-    node_shift = math.e ** (LOG_STEP * (ones - at_one))
+    node_shift = LOG_STEP * (ones - at_one)
 
     with ExitStack() as ctx:
         keep = ctx.enter_context(tc.tile_pool(name="keep", bufs=1))
+        late = ctx.enter_context(tc.tile_pool(name="late", bufs=1))
         psum = ctx.enter_context(tc.psum_pool(name="psum", bufs=1))
 
         offs_sb = keep.tile([P, S // 16], U16, name="offs_sb")
         pro_sb = keep.tile([P, V // 16], U16, name="pro_sb")
         xs = keep.tile([P, T], U8, name="xs", align_bytes=64)
-        es = keep.tile([P, W], U8, name="es", align_bytes=64)
-        step_a = keep.tile([P, nodes], F32, name="step_a", tag="bytes_a", align_bytes=64)
-        step_b = keep.tile([P, nodes], F32, name="step_b", tag="bytes_b", align_bytes=64)
-        start = keep.tile([P, 1], F32, name="start", tag="bytes_c", align_bytes=64)
-        steps = keep.tile([P, nodes], F32, name="steps", tag="bytes_d", align_bytes=64)
-        grid0 = keep.tile([P, nodes], F32, name="grid0")
+        es = keep.tile([P, W], U8, name="es", tag="after_es", align_bytes=64)
+        inv_row = keep.tile([P, W], F32, name="inv_row", tag="after_inv", align_bytes=64)
+        steps = late.tile([P, nodes], F32, name="steps", offset=W_HALF_BYTES, align_bytes=64)
         grid = keep.tile([P, ones + nodes], F32, name="grid")
-
-        nc.gpsimd.memset(xs[:].bitcast(I32), 0)
-        nc.gpsimd.memset(step_a[:], LOG_STEP / 2)
-        nc.vector.memset(step_b[:], LOG_STEP / 2)
-        nc.vector.memset(start[:], -LOG_STEP * (LOG_BELOW + 1))
-        nc.vector.tensor_tensor_scan(steps[:], step_a[:], step_b[:], start[:], ALU.add, ALU.add)
-        inv_row = keep.tile([P, W], F32, name="inv_row", tag="bytes_c", align_bytes=64)
-        nc.vector.memset(inv_row[:, 0:INV_SPLIT], 0.0)
-        nc.gpsimd.memset(inv_row[:, INV_SPLIT:], 0.0)
-        nc.gpsimd.memset(es[:].bitcast(I32), 0)
-        nc.scalar.activation(grid0[:], steps[:], ACT.Exp)
-        nc.vector.memset(grid[:, 0:ones], -32.0)
-        nc.vector.tensor_scalar(grid[:, ones:], grid0[:], node_shift, None, ALU.mult)
         ident = keep.tile([P, P], F32, name="ident", align_bytes=64)
+
+        nc.vector.memset(xs[:, 0 : T // 2].bitcast(I32), 0)
+        nc.gpsimd.memset(xs[:, T // 2 :].bitcast(I32), 0)
+        nc.gpsimd.memset(es[:].bitcast(I32), 0)
+        nc.vector.memset(inv_row[0 : P - 1, 0:INV_SPLIT], 0.0)
+        nc.gpsimd.iota(steps[:], [[1, nodes]], base=-LOG_BELOW, channel_multiplier=0, allow_small_or_imprecise_dtypes=True)
+        nc.gpsimd.memset(inv_row[0 : P - 1, INV_SPLIT:], 0.0)
+        nc.gpsimd.memset(grid[:, 0:ones], -32.0)
         make_identity(nc, ident[:])
 
-        w_raw = [keep.tile([P, PACK, H // 2], F32, name=f"w_raw{u}", tag=tag, align_bytes=64) for u, tag in enumerate(("bytes_a", "bytes_b"))]
+        nc.scalar.activation(grid[:, ones:], steps[:], ACT.Exp, bias=node_shift, scale=LOG_STEP)
+
+        w_raw = [keep.tile([P, PACK, H // 2], F32, name="w_raw0", align_bytes=64),
+                 late.tile([P, PACK, H // 2], F32, name="w_raw1", offset=0, align_bytes=64)]
         xw = keep.tile([P, T], U32, name="xw", align_bytes=64)
-        ew = keep.tile([P, W], U32, name="ew", tag="bytes_d", align_bytes=64)
+        ew = late.tile([P, W], U32, name="ew", offset=W_HALF_BYTES, align_bytes=64)
         w_rows = w1.rearrange("(p j) c -> p j c", j=PACK)
-        nc.sync.dma_start(offs_sb[:], offs)
+
+        def load_scales(tile, scales, quadrants):
+            for q in quadrants:
+                nc.sync.dma_start(tile[32 * q : 32 * q + 4, :].bitcast(I32), scales[0, 4 * q : 4 * q + 4, :].bitcast(I32))
+
         nc.sync.dma_start(pro_sb[:], pro)
+        nc.sync.dma_start(inv_row[P - 1 : P, :], inv[P - 1 : P, :])
+        nc.sync.dma_start(offs_sb[:], offs)
         nc.sync.dma_start(xw[:].bitcast(I32), x_words[0].rearrange("p n t -> p (n t)").bitcast(I32))
-        for q in range(4):
-            nc.scalar.dma_start(xs[32 * q : 32 * q + 4, :].bitcast(I32), x_scales[0, 4 * q : 4 * q + 4, :].bitcast(I32))
+        load_scales(xs, x_scales, range(3))
         nc.sync.dma_start(w_raw[0][:], w_rows[:, :, 0 : H // 2])
+        load_scales(xs, x_scales, range(3, 4))
         nc.sync.dma_start(w_raw[1][:], w_rows[:, :, H // 2 : H])
-        nc.sync.dma_start(inv_row[0:1, :], inv[0:1, :])
-        for q in range(4):
-            nc.sync.dma_start(es[32 * q : 32 * q + 4, :].bitcast(I32), e_scales[0, 4 * q : 4 * q + 4, :].bitcast(I32))
+        load_scales(es, e_scales, range(4))
         nc.sync.dma_start(ew[:].bitcast(I32), e_words[0].rearrange("p n t -> p (n t)").bitcast(I32))
 
-        xsg = keep.tile([P, S], U8, name="xsg", align_bytes=64)
-        esg = keep.tile([P, V], U8, name="esg", align_bytes=64)
-        xwg = keep.tile([P, S], U32, name="xwg", align_bytes=64)
-        ewg = keep.tile([P, V], U32, name="ewg", align_bytes=64)
         invg = keep.tile([P, V], F32, name="invg", align_bytes=64)
-        nc.vector.tensor_copy(xsg[:], xs[:].indirect(offs_sb[:]))
-        nc.vector.tensor_copy(xwg[:], xw[:].indirect(offs_sb[:]))
         nc.vector.tensor_copy(invg[:], inv_row[:].indirect(pro_sb[:]))
-        for u in range(2):
-            warm = psum.tile([P, S], F32, name=f"warm{u}", tag="yp", bufs=2)
-            nc.tensor.matmul_mx(out=warm[:], lhsT=xwg[:, 0:P].bitcast(FP8X4), lhsT_scale=xsg[:, 0:P],
-                                rhs=xwg[:].bitcast(FP8X4), rhs_scale=xsg[:], start=True, stop=True)
+        xsg = keep.tile([P, S], U8, name="xsg", align_bytes=64)
+        xwg = keep.tile([P, S], U32, name="xwg", tag="after_inv", align_bytes=64)
+        nc.vector.tensor_copy(xwg[:], xw[:].indirect(offs_sb[:]))
+        nc.vector.tensor_copy(xsg[:], xs[:].indirect(offs_sb[:]))
+        esg = keep.tile([P, V], U8, name="esg", align_bytes=64)
+        nc.vector.tensor_copy(esg[:], es[:].indirect(pro_sb[:]))
 
         wg = keep.tile([P, PACK, P, PACK], BF16, name="wg", align_bytes=64)
         for u in range(2):
@@ -101,27 +98,27 @@ def tile_picked_yphi_log_p_kernel(tc, x_words, x_scales, w1, e_words, e_scales, 
                 w_raw[u][:].rearrange("p j (m t) -> p m t j", t=PACK),
             )
         wc = keep.tile([P, H], U32, name="wc", align_bytes=64)
-        ws = keep.tile([P, H], U8, name="ws", align_bytes=64)
+        ws = keep.tile([P, H], U8, name="ws", tag="after_es", align_bytes=64)
         nc.vector.quantize_mx(out=wc[:].bitcast(FP8X4), scales=ws[:], in_=wg[:].rearrange("p t m j -> p (t m j)"))
-        nc.vector.tensor_copy(esg[:], es[:].indirect(pro_sb[:]))
+        ewg = keep.tile([P, V], U32, name="ewg", align_bytes=64)
         nc.vector.tensor_copy(ewg[:], ew[:].indirect(pro_sb[:]))
 
         turned = psum.tile([P, V // P, P], F32, name="turned")
         for c in range(V // P):
             nc.tensor.transpose(turned[:, c, :], invg[:, c * P : (c + 1) * P], ident[:])
-        inv_col = keep.tile([P, V // P], F32, name="inv_col", tag="bytes_b", align_bytes=64)
-        nc.scalar.copy(inv_col[:], turned[:, :, 0])
+        inv_col = keep.tile([P, V // P], F32, name="inv_col", align_bytes=64)
+        nc.scalar.copy(inv_col[:], turned[:, :, P - 1])
         spread = psum.tile([P, V], F32, name="spread")
         for c in range(V // P):
             nc.tensor.transpose(spread[:, c * P : (c + 1) * P], inv_col[:, c : c + 1].to_broadcast([P, P]), ident[:])
-        inv_all = keep.tile([P, V], F32, name="inv_all", align_bytes=64)
+        inv_all = late.tile([P, V], F32, name="inv_all", offset=0, align_bytes=64)
         nc.scalar.copy(inv_all[:], spread[:])
 
         hc = keep.tile([P, S], U32, name="hc", align_bytes=64)
-        hs = keep.tile([P, S], U8, name="hs", tag="bytes_d", align_bytes=64)
+        hs = late.tile([P, S], U8, name="hs", offset=W_HALF_BYTES, align_bytes=64)
         for b in range(BLOCKS):
             cols = slice(b * P, (b + 1) * P)
-            hp = psum.tile([P, PACK, P], F32, name=f"hp{b}", tag="hp", bufs=4)
+            hp = psum.tile([P, PACK, P], F32, name=f"hp{b}", tag="acc", bufs=4)
             for t in range(PACK):
                 tcols = slice(t * P, (t + 1) * P)
                 nc.tensor.matmul_mx(out=hp[:, t, :], lhsT=wc[:, tcols].bitcast(FP8X4), lhsT_scale=ws[:, tcols],

@@ -22,6 +22,7 @@ BLOCKS = S // P
 LOG_STEP = 0.375
 LOG_BELOW = 80
 LOG_ABOVE = 8
+M_SPLIT = 32
 W_HALF_BYTES = PACK * (H // 2) * 4
 INV_SPLIT = 1408
 
@@ -88,19 +89,27 @@ def tile_picked_yphi_log_p_kernel(tc, x_words, x_scales, w1, e_words, e_scales, 
         xwg = keep.tile([P, S], U32, name="xwg", tag="after_inv", align_bytes=64)
         nc.vector.tensor_copy(xwg[:], xw[:].indirect(offs_sb[:]))
         nc.vector.tensor_copy(xsg[:], xs[:].indirect(offs_sb[:]))
-        esg = keep.tile([P, V], U8, name="esg", align_bytes=64)
-        nc.vector.tensor_copy(esg[:], es[:].indirect(pro_sb[:]))
 
-        wg = keep.tile([P, PACK, P, PACK], BF16, name="wg", align_bytes=64)
+        warm = psum.tile([P, S], F32, name="warm")
         for u in range(2):
-            nc.scalar.copy(
-                wg[:, :, u * P // 2 : (u + 1) * P // 2, :].rearrange("p t m j -> p m t j"),
-                w_raw[u][:].rearrange("p j (m t) -> p m t j", t=PACK),
+            nc.tensor.matmul_mx(out=warm[:], lhsT=xwg[:, 0:P].bitcast(FP8X4), lhsT_scale=xsg[:, 0:P],
+                                rhs=xwg[:].bitcast(FP8X4), rhs_scale=xsg[:], start=True, stop=True)
+
+        wg = keep.tile([P, PACK, P, PACK], BF16, name="wg", tag="after_wg", align_bytes=64)
+        for copy, u, lo, hi in ((nc.scalar.copy, 0, 0, 64), (nc.scalar.copy, 1, 0, M_SPLIT), (nc.vector.tensor_copy, 1, M_SPLIT, 64)):
+            copy(
+                wg[:, :, 64 * u + lo : 64 * u + hi, :].rearrange("p t m j -> p m t j"),
+                w_raw[u][:, :, PACK * lo : PACK * hi].rearrange("p j (m t) -> p m t j", t=PACK),
             )
         wc = keep.tile([P, H], U32, name="wc", align_bytes=64)
-        ws = keep.tile([P, H], U8, name="ws", tag="after_es", align_bytes=64)
-        nc.vector.quantize_mx(out=wc[:].bitcast(FP8X4), scales=ws[:], in_=wg[:].rearrange("p t m j -> p (t m j)"))
-        ewg = keep.tile([P, V], U32, name="ewg", align_bytes=64)
+        ws = keep.tile([P, H], U8, name="ws", align_bytes=64)
+        for u in range(2):
+            half = slice(u * H // 2, (u + 1) * H // 2)
+            nc.vector.quantize_mx(out=wc[:, half].bitcast(FP8X4), scales=ws[:, half],
+                                  in_=wg[:, 2 * u : 2 * u + 2].rearrange("p t m j -> p (t m j)"))
+        esg = keep.tile([P, V], U8, name="esg", tag="after_wg", align_bytes=64)
+        nc.vector.tensor_copy(esg[:], es[:].indirect(pro_sb[:]))
+        ewg = keep.tile([P, V], U32, name="ewg", tag="after_es", align_bytes=64)
         nc.vector.tensor_copy(ewg[:], ew[:].indirect(pro_sb[:]))
 
         turned = psum.tile([P, V // P, P], F32, name="turned")
@@ -127,10 +136,10 @@ def tile_picked_yphi_log_p_kernel(tc, x_words, x_scales, w1, e_words, e_scales, 
             nc.scalar.copy(hb[:], hp[:].rearrange("p t n -> p n t"))
             nc.vector.quantize_mx(out=hc[:, cols].bitcast(FP8X4), scales=hs[:, cols], in_=hb[:].rearrange("p n t -> p (n t)"))
 
-        junk = [keep.tile([P, V], F32, name=f"junk{u}", align_bytes=64) for u in range(2)]
+        junk = keep.tile([P, V], F32, name="junk", align_bytes=64)
         for b in range(BLOCKS):
             cols = slice(b * P, (b + 1) * P)
-            yp = psum.tile([P, V], F32, name=f"yp{b}", tag="yp", bufs=2)
+            yp = psum.tile([P, V], F32, name=f"yp{b}", tag="acc", bufs=4)
             nc.tensor.matmul_mx(out=yp[:], lhsT=hc[:, cols].bitcast(FP8X4), lhsT_scale=hs[:, cols],
                                 rhs=ewg[:].bitcast(FP8X4), rhs_scale=esg[:], start=True, stop=True)
             z = keep.tile([P, V], F32, name=f"z{b}", align_bytes=64)
@@ -138,16 +147,23 @@ def tile_picked_yphi_log_p_kernel(tc, x_words, x_scales, w1, e_words, e_scales, 
             neg_max = keep.tile([P, 1], F32, name=f"neg_max{b}")
             nc.vector.tensor_reduce(neg_max[:], z[:], AXIS.X, ALU.max, negate=True)
             total = keep.tile([P, 1], F32, name=f"total{b}")
-            nc.scalar.activation(junk[b % 2][:], z[:], ACT.Exp, bias=neg_max[:], accum_out=total[:])
+            nc.scalar.activation(junk[:], z[:], ACT.Exp, bias=neg_max[:], accum_out=total[:])
             log_steps = keep.tile([P, 1], F32, name=f"log_steps{b}")
-            nc.scalar.activation(junk[b % 2][:, 0 : ones + nodes], grid[:], ACT.Tanh, scale=total[:], accum_out=log_steps[:])
+            nc.scalar.activation(junk[:, 0 : ones + nodes], grid[:], ACT.Tanh, scale=total[:], accum_out=log_steps[:])
             res = keep.tile([P, V], F32, name=f"res{b}", align_bytes=64)
             if b < BLOCKS - 2:
                 shift = keep.tile([P, 1], F32, name=f"shift{b}")
-                nc.scalar.activation(shift[:], log_steps[:], ACT.Identity, bias=neg_max[:], scale=-LOG_STEP)
+                nc.gpsimd.tensor_scalar(shift[:], log_steps[:], -LOG_STEP, neg_max[:], ALU.mult, ALU.add)
                 nc.gpsimd.tensor_scalar(res[:], z[:], shift[:], 1.0, ALU.add, ALU.mult)
             else:
                 centred = keep.tile([P, V], F32, name=f"centred{b}", align_bytes=64)
                 nc.vector.tensor_scalar(centred[:], z[:], neg_max[:], 1.0 / LOG_STEP, ALU.add, ALU.mult)
-                nc.vector.tensor_scalar(res[:], centred[:], log_steps[:], LOG_STEP, ALU.subtract, ALU.mult)
-            nc.sync.dma_start(out[cols, :], res[:])
+                if b < BLOCKS - 1:
+                    nc.vector.tensor_scalar(res[:], centred[:], log_steps[:], LOG_STEP, ALU.subtract, ALU.mult)
+            if b < BLOCKS - 1:
+                nc.sync.dma_start(out[cols, :], res[:])
+            else:
+                for u, queue in enumerate((nc.scalar, nc.sync)):
+                    half = slice(u * V // 2, (u + 1) * V // 2)
+                    nc.vector.tensor_scalar(res[:, half], centred[:, half], log_steps[:], LOG_STEP, ALU.subtract, ALU.mult)
+                    queue.dma_start(out[cols, half], res[:, half])

@@ -90,7 +90,7 @@ def tile_picked_yphi_log_p_kernel(tc, x_words, x_scales, w1, e_words, e_scales, 
         nc.vector.tensor_copy(xwg[:], xw[:].indirect(offs_sb[:]))
         nc.vector.tensor_copy(xsg[:], xs[:].indirect(offs_sb[:]))
 
-        warm = psum.tile([P, S], F32, name="warm")
+        warm = psum.tile([P, S], F32, name="warm", tag="yp", bufs=2)
         for u in range(2):
             nc.tensor.matmul_mx(out=warm[:], lhsT=xwg[:, 0:P].bitcast(FP8X4), lhsT_scale=xsg[:, 0:P],
                                 rhs=xwg[:].bitcast(FP8X4), rhs_scale=xsg[:], start=True, stop=True)
@@ -116,7 +116,7 @@ def tile_picked_yphi_log_p_kernel(tc, x_words, x_scales, w1, e_words, e_scales, 
         for c in range(V // P):
             nc.tensor.transpose(turned[:, c, :], invg[:, c * P : (c + 1) * P], ident[:])
         inv_col = keep.tile([P, V // P], F32, name="inv_col", align_bytes=64)
-        nc.scalar.copy(inv_col[:], turned[:, :, P - 1])
+        nc.vector.tensor_copy(inv_col[:], turned[:, :, P - 1])
         spread = psum.tile([P, V], F32, name="spread")
         for c in range(V // P):
             nc.tensor.transpose(spread[:, c * P : (c + 1) * P], inv_col[:, c : c + 1].to_broadcast([P, P]), ident[:])
@@ -136,10 +136,10 @@ def tile_picked_yphi_log_p_kernel(tc, x_words, x_scales, w1, e_words, e_scales, 
             nc.scalar.copy(hb[:], hp[:].rearrange("p t n -> p n t"))
             nc.vector.quantize_mx(out=hc[:, cols].bitcast(FP8X4), scales=hs[:, cols], in_=hb[:].rearrange("p n t -> p (n t)"))
 
-        junk = keep.tile([P, V], F32, name="junk", align_bytes=64)
+        junk = [keep.tile([P, V], F32, name=f"junk{u}", align_bytes=64) for u in range(2)]
         for b in range(BLOCKS):
             cols = slice(b * P, (b + 1) * P)
-            yp = psum.tile([P, V], F32, name=f"yp{b}", tag="acc", bufs=4)
+            yp = psum.tile([P, V], F32, name=f"yp{b}", tag="yp", bufs=2)
             nc.tensor.matmul_mx(out=yp[:], lhsT=hc[:, cols].bitcast(FP8X4), lhsT_scale=hs[:, cols],
                                 rhs=ewg[:].bitcast(FP8X4), rhs_scale=esg[:], start=True, stop=True)
             z = keep.tile([P, V], F32, name=f"z{b}", align_bytes=64)
@@ -147,23 +147,16 @@ def tile_picked_yphi_log_p_kernel(tc, x_words, x_scales, w1, e_words, e_scales, 
             neg_max = keep.tile([P, 1], F32, name=f"neg_max{b}")
             nc.vector.tensor_reduce(neg_max[:], z[:], AXIS.X, ALU.max, negate=True)
             total = keep.tile([P, 1], F32, name=f"total{b}")
-            nc.scalar.activation(junk[:], z[:], ACT.Exp, bias=neg_max[:], accum_out=total[:])
+            nc.scalar.activation(junk[b % 2][:], z[:], ACT.Exp, bias=neg_max[:], accum_out=total[:])
             log_steps = keep.tile([P, 1], F32, name=f"log_steps{b}")
-            nc.scalar.activation(junk[:, 0 : ones + nodes], grid[:], ACT.Tanh, scale=total[:], accum_out=log_steps[:])
+            nc.scalar.activation(junk[b % 2][:, 0 : ones + nodes], grid[:], ACT.Tanh, scale=total[:], accum_out=log_steps[:])
             res = keep.tile([P, V], F32, name=f"res{b}", align_bytes=64)
             if b < BLOCKS - 2:
                 shift = keep.tile([P, 1], F32, name=f"shift{b}")
-                nc.gpsimd.tensor_scalar(shift[:], log_steps[:], -LOG_STEP, neg_max[:], ALU.mult, ALU.add)
+                nc.scalar.activation(shift[:], log_steps[:], ACT.Identity, bias=neg_max[:], scale=-LOG_STEP)
                 nc.gpsimd.tensor_scalar(res[:], z[:], shift[:], 1.0, ALU.add, ALU.mult)
             else:
                 centred = keep.tile([P, V], F32, name=f"centred{b}", align_bytes=64)
                 nc.vector.tensor_scalar(centred[:], z[:], neg_max[:], 1.0 / LOG_STEP, ALU.add, ALU.mult)
-                if b < BLOCKS - 1:
-                    nc.vector.tensor_scalar(res[:], centred[:], log_steps[:], LOG_STEP, ALU.subtract, ALU.mult)
-            if b < BLOCKS - 1:
-                nc.sync.dma_start(out[cols, :], res[:])
-            else:
-                for u, queue in enumerate((nc.scalar, nc.sync)):
-                    half = slice(u * V // 2, (u + 1) * V // 2)
-                    nc.vector.tensor_scalar(res[:, half], centred[:, half], log_steps[:], LOG_STEP, ALU.subtract, ALU.mult)
-                    queue.dma_start(out[cols, half], res[:, half])
+                nc.vector.tensor_scalar(res[:], centred[:], log_steps[:], LOG_STEP, ALU.subtract, ALU.mult)
+            nc.sync.dma_start(out[cols, :], res[:])

@@ -20,8 +20,8 @@ PACK = 4
 K, T, S, H, V, W = 512, 1024, 512, 512, 512, 2048
 BLOCKS = S // P
 LOG_STEP = 0.375
-LOG_BELOW = 80
-LOG_ABOVE = 8
+LOG_BELOW = 76
+LOG_ABOVE = 9
 M_SPLIT = 32
 W_HALF_BYTES = PACK * (H // 2) * 4
 INV_SPLIT = 1408
@@ -33,9 +33,8 @@ BYTES = K * T + K * T // 32 + 4 * K * H + H * W + H * W // 32 + 4 * W + 2 * P * 
 def tile_picked_yphi_log_p_kernel(tc, x_words, x_scales, w1, e_words, e_scales, inv, offs, pro, out):
     nc = tc.nc
     nodes = LOG_BELOW + LOG_ABOVE + 1
-    at_one = sum(math.tanh(math.e ** (LOG_STEP * j)) for j in range(-LOG_BELOW, LOG_ABOVE + 1))
-    ones = round(at_one)
-    node_shift = LOG_STEP * (ones - at_one)
+    sum_at_one = LOG_STEP * sum(math.e ** -(math.e ** (LOG_STEP * j)) for j in range(-LOG_BELOW, LOG_ABOVE + 1))
+    log_of_step = math.log10(LOG_STEP) / math.log10(math.e)
 
     with ExitStack() as ctx:
         keep = ctx.enter_context(tc.tile_pool(name="keep", bufs=1))
@@ -48,7 +47,8 @@ def tile_picked_yphi_log_p_kernel(tc, x_words, x_scales, w1, e_words, e_scales, 
         es = keep.tile([P, W], U8, name="es", tag="after_es", align_bytes=64)
         inv_row = keep.tile([P, W], F32, name="inv_row", tag="after_inv", align_bytes=64)
         steps = late.tile([P, nodes], F32, name="steps", offset=W_HALF_BYTES, align_bytes=64)
-        grid = keep.tile([P, ones + nodes], F32, name="grid")
+        grid = keep.tile([P, nodes], F32, name="grid")
+        nodes_up = keep.tile([P, nodes], F32, name="nodes_up")
         ident = keep.tile([P, P], F32, name="ident", align_bytes=64)
 
         nc.vector.memset(xs[:, 0 : T // 2].bitcast(I32), 0)
@@ -57,10 +57,10 @@ def tile_picked_yphi_log_p_kernel(tc, x_words, x_scales, w1, e_words, e_scales, 
         nc.vector.memset(inv_row[0 : P - 1, 0:INV_SPLIT], 0.0)
         nc.gpsimd.iota(steps[:], [[1, nodes]], base=-LOG_BELOW, channel_multiplier=0, allow_small_or_imprecise_dtypes=True)
         nc.gpsimd.memset(inv_row[0 : P - 1, INV_SPLIT:], 0.0)
-        nc.gpsimd.memset(grid[:, 0:ones], -32.0)
         make_identity(nc, ident[:])
 
-        nc.scalar.activation(grid[:, ones:], steps[:], ACT.Exp, bias=node_shift, scale=LOG_STEP)
+        nc.scalar.activation(nodes_up[:], steps[:], ACT.Exp, scale=LOG_STEP)
+        nc.scalar.mul(grid[:], nodes_up[:], -1.0)
 
         w_raw = [keep.tile([P, PACK, H // 2], F32, name="w_raw0", align_bytes=64),
                  late.tile([P, PACK, H // 2], F32, name="w_raw1", offset=0, align_bytes=64)]
@@ -136,6 +136,14 @@ def tile_picked_yphi_log_p_kernel(tc, x_words, x_scales, w1, e_words, e_scales, 
             nc.scalar.copy(hb[:], hp[:].rearrange("p t n -> p n t"))
             nc.vector.quantize_mx(out=hc[:, cols].bitcast(FP8X4), scales=hs[:, cols], in_=hb[:].rearrange("p n t -> p (n t)"))
 
+        rows = []
+
+        def finish(b):
+            z, base, rest = rows[b]
+            res = keep.tile([P, V], F32, name=f"res{b}", align_bytes=64)
+            nc.vector.tensor_scalar(res[:], z[:], base[:], rest[:], ALU.add, ALU.add)
+            nc.sync.dma_start(out[b * P : (b + 1) * P, :], res[:])
+
         junk = [keep.tile([P, V], F32, name=f"junk{u}", align_bytes=64) for u in range(2)]
         for b in range(BLOCKS):
             cols = slice(b * P, (b + 1) * P)
@@ -148,15 +156,11 @@ def tile_picked_yphi_log_p_kernel(tc, x_words, x_scales, w1, e_words, e_scales, 
             nc.vector.tensor_reduce(neg_max[:], z[:], AXIS.X, ALU.max, negate=True)
             total = keep.tile([P, 1], F32, name=f"total{b}")
             nc.scalar.activation(junk[b % 2][:], z[:], ACT.Exp, bias=neg_max[:], accum_out=total[:])
-            log_steps = keep.tile([P, 1], F32, name=f"log_steps{b}")
-            nc.scalar.activation(junk[b % 2][:, 0 : ones + nodes], grid[:], ACT.Tanh, scale=total[:], accum_out=log_steps[:])
-            res = keep.tile([P, V], F32, name=f"res{b}", align_bytes=64)
-            if b < BLOCKS - 2:
-                shift = keep.tile([P, 1], F32, name=f"shift{b}")
-                nc.scalar.activation(shift[:], log_steps[:], ACT.Identity, bias=neg_max[:], scale=-LOG_STEP)
-                nc.gpsimd.tensor_scalar(res[:], z[:], shift[:], 1.0, ALU.add, ALU.mult)
-            else:
-                centred = keep.tile([P, V], F32, name=f"centred{b}", align_bytes=64)
-                nc.vector.tensor_scalar(centred[:], z[:], neg_max[:], 1.0 / LOG_STEP, ALU.add, ALU.mult)
-                nc.vector.tensor_scalar(res[:], centred[:], log_steps[:], LOG_STEP, ALU.subtract, ALU.mult)
-            nc.sync.dma_start(out[cols, :], res[:])
+            base = keep.tile([P, 1], F32, name=f"base{b}")
+            nc.scalar.activation(base[:], neg_max[:], ACT.Identity, bias=-sum_at_one)
+            rest = keep.tile([P, 1], F32, name=f"rest{b}")
+            nc.scalar.activation(junk[b % 2][:, 0:nodes], grid[:], ACT.Exp, bias=log_of_step, scale=total[:], accum_out=rest[:])
+            rows.append((z, base, rest))
+
+        for b in range(BLOCKS):
+            finish(b)

@@ -17,14 +17,19 @@ AXIS = mybir.AxisListType
 
 P = 128
 PACK = 4
+QUADRANTS = 4
 K, T, S, H, V, W = 512, 1024, 512, 512, 512, 2048
 BLOCKS = S // P
+M_HALF = P // 2
+
 LOG_STEP = 0.375
 LOG_BELOW = 76
 LOG_ABOVE = 9
+NODES = LOG_BELOW + LOG_ABOVE + 1
+
 M_SPLIT = 32
-W_HALF_BYTES = PACK * (H // 2) * 4
 INV_SPLIT = 1408
+W_HALF_BYTES = PACK * (H // 2) * 4
 
 FLOPS = 2 * K * H * S + 2 * H * S * V
 BYTES = K * T + K * T // 32 + 4 * K * H + H * W + H * W // 32 + 4 * W + 2 * P * (S + V) // 16 + 4 * S * V
@@ -32,13 +37,12 @@ BYTES = K * T + K * T // 32 + 4 * K * H + H * W + H * W // 32 + 4 * W + 2 * P * 
 
 def tile_picked_yphi_log_p_kernel(tc, x_words, x_scales, w1, e_words, e_scales, inv, offs, pro, out):
     nc = tc.nc
-    nodes = LOG_BELOW + LOG_ABOVE + 1
     sum_at_one = LOG_STEP * sum(math.e ** -(math.e ** (LOG_STEP * j)) for j in range(-LOG_BELOW, LOG_ABOVE + 1))
     log_of_step = math.log10(LOG_STEP) / math.log10(math.e)
 
     with ExitStack() as ctx:
         keep = ctx.enter_context(tc.tile_pool(name="keep", bufs=1))
-        late = ctx.enter_context(tc.tile_pool(name="late", bufs=1))
+        shared = ctx.enter_context(tc.tile_pool(name="shared", bufs=1))
         psum = ctx.enter_context(tc.psum_pool(name="psum", bufs=1))
 
         offs_sb = keep.tile([P, S // 16], U16, name="offs_sb")
@@ -46,16 +50,16 @@ def tile_picked_yphi_log_p_kernel(tc, x_words, x_scales, w1, e_words, e_scales, 
         xs = keep.tile([P, T], U8, name="xs", align_bytes=64)
         es = keep.tile([P, W], U8, name="es", tag="after_es", align_bytes=64)
         inv_row = keep.tile([P, W], F32, name="inv_row", tag="after_inv", align_bytes=64)
-        steps = late.tile([P, nodes], F32, name="steps", offset=W_HALF_BYTES, align_bytes=64)
-        grid = keep.tile([P, nodes], F32, name="grid")
-        nodes_up = keep.tile([P, nodes], F32, name="nodes_up")
+        steps = shared.tile([P, NODES], F32, name="steps", offset=W_HALF_BYTES, align_bytes=64)
+        grid = keep.tile([P, NODES], F32, name="grid")
+        nodes_up = keep.tile([P, NODES], F32, name="nodes_up")
         ident = keep.tile([P, P], F32, name="ident", align_bytes=64)
 
         nc.vector.memset(xs[:, 0 : T // 2].bitcast(I32), 0)
         nc.gpsimd.memset(xs[:, T // 2 :].bitcast(I32), 0)
         nc.gpsimd.memset(es[:].bitcast(I32), 0)
         nc.vector.memset(inv_row[0 : P - 1, 0:INV_SPLIT], 0.0)
-        nc.gpsimd.iota(steps[:], [[1, nodes]], base=-LOG_BELOW, channel_multiplier=0, allow_small_or_imprecise_dtypes=True)
+        nc.gpsimd.iota(steps[:], [[1, NODES]], base=-LOG_BELOW, channel_multiplier=0, allow_small_or_imprecise_dtypes=True)
         nc.gpsimd.memset(inv_row[0 : P - 1, INV_SPLIT:], 0.0)
         make_identity(nc, ident[:])
 
@@ -63,9 +67,9 @@ def tile_picked_yphi_log_p_kernel(tc, x_words, x_scales, w1, e_words, e_scales, 
         nc.scalar.mul(grid[:], nodes_up[:], -1.0)
 
         w_raw = [keep.tile([P, PACK, H // 2], F32, name="w_raw0", align_bytes=64),
-                 late.tile([P, PACK, H // 2], F32, name="w_raw1", offset=0, align_bytes=64)]
+                 shared.tile([P, PACK, H // 2], F32, name="w_raw1", offset=0, align_bytes=64)]
         xw = keep.tile([P, T], U32, name="xw", align_bytes=64)
-        ew = late.tile([P, W], U32, name="ew", offset=W_HALF_BYTES, align_bytes=64)
+        ew = shared.tile([P, W], U32, name="ew", offset=W_HALF_BYTES, align_bytes=64)
         w_rows = w1.rearrange("(p j) c -> p j c", j=PACK)
 
         def load_scales(tile, scales, quadrants):
@@ -73,14 +77,14 @@ def tile_picked_yphi_log_p_kernel(tc, x_words, x_scales, w1, e_words, e_scales, 
                 nc.sync.dma_start(tile[32 * q : 32 * q + 4, :].bitcast(I32), scales[0, 4 * q : 4 * q + 4, :].bitcast(I32))
 
         nc.sync.dma_start(pro_sb[:], pro)
-        nc.sync.dma_start(inv_row[P - 1 : P, :], inv[P - 1 : P, :])
+        nc.sync.dma_start(inv_row[P - 1 : P, :], inv[0:1, :])
         nc.sync.dma_start(offs_sb[:], offs)
         nc.sync.dma_start(xw[:].bitcast(I32), x_words[0].rearrange("p n t -> p (n t)").bitcast(I32))
-        load_scales(xs, x_scales, range(3))
+        load_scales(xs, x_scales, range(QUADRANTS - 1))
         nc.sync.dma_start(w_raw[0][:], w_rows[:, :, 0 : H // 2])
-        load_scales(xs, x_scales, range(3, 4))
+        load_scales(xs, x_scales, range(QUADRANTS - 1, QUADRANTS))
         nc.sync.dma_start(w_raw[1][:], w_rows[:, :, H // 2 : H])
-        load_scales(es, e_scales, range(4))
+        load_scales(es, e_scales, range(QUADRANTS))
         nc.sync.dma_start(ew[:].bitcast(I32), e_words[0].rearrange("p n t -> p (n t)").bitcast(I32))
 
         invg = keep.tile([P, V], F32, name="invg", align_bytes=64)
@@ -90,15 +94,11 @@ def tile_picked_yphi_log_p_kernel(tc, x_words, x_scales, w1, e_words, e_scales, 
         nc.vector.tensor_copy(xwg[:], xw[:].indirect(offs_sb[:]))
         nc.vector.tensor_copy(xsg[:], xs[:].indirect(offs_sb[:]))
 
-        warm = psum.tile([P, S], F32, name="warm", tag="yp", bufs=2)
-        for u in range(2):
-            nc.tensor.matmul_mx(out=warm[:], lhsT=xwg[:, 0:P].bitcast(FP8X4), lhsT_scale=xsg[:, 0:P],
-                                rhs=xwg[:].bitcast(FP8X4), rhs_scale=xsg[:], start=True, stop=True)
-
         wg = keep.tile([P, PACK, P, PACK], BF16, name="wg", tag="after_wg", align_bytes=64)
-        for copy, u, lo, hi in ((nc.scalar.copy, 0, 0, 64), (nc.scalar.copy, 1, 0, M_SPLIT), (nc.vector.tensor_copy, 1, M_SPLIT, 64)):
+        shares = ((nc.scalar.copy, 0, 0, M_HALF), (nc.scalar.copy, 1, 0, M_SPLIT), (nc.vector.tensor_copy, 1, M_SPLIT, M_HALF))
+        for copy, u, lo, hi in shares:
             copy(
-                wg[:, :, 64 * u + lo : 64 * u + hi, :].rearrange("p t m j -> p m t j"),
+                wg[:, :, M_HALF * u + lo : M_HALF * u + hi, :].rearrange("p t m j -> p m t j"),
                 w_raw[u][:, :, PACK * lo : PACK * hi].rearrange("p j (m t) -> p m t j", t=PACK),
             )
         wc = keep.tile([P, H], U32, name="wc", align_bytes=64)
@@ -107,6 +107,7 @@ def tile_picked_yphi_log_p_kernel(tc, x_words, x_scales, w1, e_words, e_scales, 
             half = slice(u * H // 2, (u + 1) * H // 2)
             nc.vector.quantize_mx(out=wc[:, half].bitcast(FP8X4), scales=ws[:, half],
                                   in_=wg[:, 2 * u : 2 * u + 2].rearrange("p t m j -> p (t m j)"))
+
         esg = keep.tile([P, V], U8, name="esg", tag="after_wg", align_bytes=64)
         nc.vector.tensor_copy(esg[:], es[:].indirect(pro_sb[:]))
         ewg = keep.tile([P, V], U32, name="ewg", tag="after_es", align_bytes=64)
@@ -120,14 +121,14 @@ def tile_picked_yphi_log_p_kernel(tc, x_words, x_scales, w1, e_words, e_scales, 
         spread = psum.tile([P, V], F32, name="spread")
         for c in range(V // P):
             nc.tensor.transpose(spread[:, c * P : (c + 1) * P], inv_col[:, c : c + 1].to_broadcast([P, P]), ident[:])
-        inv_all = late.tile([P, V], F32, name="inv_all", offset=0, align_bytes=64)
+        inv_all = shared.tile([P, V], F32, name="inv_all", offset=0, align_bytes=64)
         nc.scalar.copy(inv_all[:], spread[:])
 
         hc = keep.tile([P, S], U32, name="hc", align_bytes=64)
-        hs = late.tile([P, S], U8, name="hs", offset=W_HALF_BYTES, align_bytes=64)
+        hs = shared.tile([P, S], U8, name="hs", offset=W_HALF_BYTES, align_bytes=64)
         for b in range(BLOCKS):
             cols = slice(b * P, (b + 1) * P)
-            hp = psum.tile([P, PACK, P], F32, name=f"hp{b}", tag="acc", bufs=4)
+            hp = psum.tile([P, PACK, P], F32, name=f"hp{b}", tag="acc", bufs=BLOCKS)
             for t in range(PACK):
                 tcols = slice(t * P, (t + 1) * P)
                 nc.tensor.matmul_mx(out=hp[:, t, :], lhsT=wc[:, tcols].bitcast(FP8X4), lhsT_scale=ws[:, tcols],
@@ -137,14 +138,7 @@ def tile_picked_yphi_log_p_kernel(tc, x_words, x_scales, w1, e_words, e_scales, 
             nc.vector.quantize_mx(out=hc[:, cols].bitcast(FP8X4), scales=hs[:, cols], in_=hb[:].rearrange("p n t -> p (n t)"))
 
         rows = []
-
-        def finish(b):
-            z, base, rest = rows[b]
-            res = keep.tile([P, V], F32, name=f"res{b}", align_bytes=64)
-            nc.vector.tensor_scalar(res[:], z[:], base[:], rest[:], ALU.add, ALU.add)
-            nc.sync.dma_start(out[b * P : (b + 1) * P, :], res[:])
-
-        junk = [keep.tile([P, V], F32, name=f"junk{u}", align_bytes=64) for u in range(2)]
+        scratch = [keep.tile([P, V], F32, name="scratch0", align_bytes=64)]
         for b in range(BLOCKS):
             cols = slice(b * P, (b + 1) * P)
             yp = psum.tile([P, V], F32, name=f"yp{b}", tag="yp", bufs=2)
@@ -155,12 +149,22 @@ def tile_picked_yphi_log_p_kernel(tc, x_words, x_scales, w1, e_words, e_scales, 
             neg_max = keep.tile([P, 1], F32, name=f"neg_max{b}")
             nc.vector.tensor_reduce(neg_max[:], z[:], AXIS.X, ALU.max, negate=True)
             total = keep.tile([P, 1], F32, name=f"total{b}")
-            nc.scalar.activation(junk[b % 2][:], z[:], ACT.Exp, bias=neg_max[:], accum_out=total[:])
+            nc.scalar.activation(scratch[b % 2][:], z[:], ACT.Exp, bias=neg_max[:], accum_out=total[:])
             base = keep.tile([P, 1], F32, name=f"base{b}")
             nc.scalar.activation(base[:], neg_max[:], ACT.Identity, bias=-sum_at_one)
-            rest = keep.tile([P, 1], F32, name=f"rest{b}")
-            nc.scalar.activation(junk[b % 2][:, 0:nodes], grid[:], ACT.Exp, bias=log_of_step, scale=total[:], accum_out=rest[:])
+            rest = keep.tile([P, 1], F32, name=f"rest{b}", tag="after_rest0" if b == 0 else f"rest{b}", align_bytes=64)
+            nc.scalar.activation(scratch[b % 2][:, 0:NODES], grid[:], ACT.Exp, bias=log_of_step, scale=total[:], accum_out=rest[:])
             rows.append((z, base, rest))
+            if b == 0:
+                shift = keep.tile([P, 1], F32, name="shift")
+                nc.scalar.activation(shift[:], rest[:], ACT.Identity, bias=base[:])
+                first = keep.tile([P, V], F32, name="res0", align_bytes=64)
+                nc.gpsimd.tensor_scalar(first[:], z[:], shift[:], 1.0, ALU.add, ALU.mult)
+                nc.sync.dma_start(out[cols, :], first[:])
+                scratch.append(keep.tile([P, V], F32, name="scratch1", tag="after_rest0", align_bytes=64))
 
-        for b in range(BLOCKS):
-            finish(b)
+        for b in range(1, BLOCKS):
+            z, base, rest = rows[b]
+            res = keep.tile([P, V], F32, name=f"res{b}", align_bytes=64)
+            nc.vector.tensor_scalar(res[:], z[:], base[:], rest[:], ALU.add, ALU.add)
+            nc.sync.dma_start(out[b * P : (b + 1) * P, :], res[:])

@@ -20,14 +20,14 @@ PACK = 4
 QUADRANTS = 4
 K, T, S, H, V, W = 512, 1024, 512, 512, 512, 2048
 BLOCKS = S // P
-M_HALF = P // 2
+W_CUTS = (0, 3 * H // 8, 3 * H // 4, H)
 
 LOG_STEP = 0.375
 LOG_BELOW = 76
 LOG_ABOVE = 9
 NODES = LOG_BELOW + LOG_ABOVE + 1
 
-M_SPLIT = 32
+ROW0 = P - 16
 INV_SPLIT = 1408
 W_HALF_BYTES = PACK * (H // 2) * 4
 
@@ -48,59 +48,65 @@ def tile_picked_yphi_log_p_kernel(tc, x_words, x_scales, w1, e_words, e_scales, 
         offs_sb = keep.tile([P, S // 16], U16, name="offs_sb")
         pro_sb = keep.tile([P, V // 16], U16, name="pro_sb")
         xs = keep.tile([P, T], U8, name="xs", align_bytes=64)
-        es = keep.tile([P, W], U8, name="es", tag="after_es", align_bytes=64)
-        inv_row = keep.tile([P, W], F32, name="inv_row", tag="after_inv", align_bytes=64)
-        steps = shared.tile([P, NODES], F32, name="steps", offset=W_HALF_BYTES, align_bytes=64)
+        es = keep.tile([P, W], U8, name="es", align_bytes=64)
+        inv_row = keep.tile([P, W], F32, name="inv_row", align_bytes=64)
+        x_plane = keep.tile([P, S], U8, name="x_plane", align_bytes=64)
+        e_plane = keep.tile([P, V], U8, name="e_plane", align_bytes=64)
+        steps = keep.tile([P, NODES], F32, name="steps")
         grid = keep.tile([P, NODES], F32, name="grid")
         nodes_up = keep.tile([P, NODES], F32, name="nodes_up")
         ident = keep.tile([P, P], F32, name="ident", align_bytes=64)
 
-        nc.vector.memset(xs[:, 0 : T // 2].bitcast(I32), 0)
-        nc.gpsimd.memset(xs[:, T // 2 :].bitcast(I32), 0)
-        nc.gpsimd.memset(es[:].bitcast(I32), 0)
+        nc.gpsimd.memset(xs[0:ROW0, :].bitcast(I32), 0)
+        nc.gpsimd.memset(x_plane[:].bitcast(I32), 0)
         nc.vector.memset(inv_row[0 : P - 1, 0:INV_SPLIT], 0.0)
         nc.gpsimd.iota(steps[:], [[1, NODES]], base=-LOG_BELOW, channel_multiplier=0, allow_small_or_imprecise_dtypes=True)
         nc.gpsimd.memset(inv_row[0 : P - 1, INV_SPLIT:], 0.0)
+        nc.gpsimd.memset(es[0:ROW0, :].bitcast(I32), 0)
+        nc.gpsimd.memset(e_plane[:].bitcast(I32), 0)
         make_identity(nc, ident[:])
 
         nc.scalar.activation(nodes_up[:], steps[:], ACT.Exp, scale=LOG_STEP)
         nc.scalar.mul(grid[:], nodes_up[:], -1.0)
 
-        w_raw = [keep.tile([P, PACK, H // 2], F32, name="w_raw0", align_bytes=64),
-                 shared.tile([P, PACK, H // 2], F32, name="w_raw1", offset=0, align_bytes=64)]
-        xw = keep.tile([P, T], U32, name="xw", align_bytes=64)
+        w_raw = [shared.tile([P, PACK, W_CUTS[1]], F32, name="w_raw0", offset=W_HALF_BYTES, align_bytes=64),
+                 keep.tile([P, PACK, W_CUTS[2] - W_CUTS[1]], F32, name="w_raw1", align_bytes=64),
+                 shared.tile([P, PACK, H - W_CUTS[2]], F32, name="w_raw2", offset=0, align_bytes=64)]
+        xw = keep.tile([P, T], U32, name="xw", tag="after_xw", align_bytes=64)
         ew = shared.tile([P, W], U32, name="ew", offset=W_HALF_BYTES, align_bytes=64)
         w_rows = w1.rearrange("(p j) c -> p j c", j=PACK)
 
-        def load_scales(tile, scales, quadrants):
-            for q in quadrants:
-                nc.sync.dma_start(tile[32 * q : 32 * q + 4, :].bitcast(I32), scales[0, 4 * q : 4 * q + 4, :].bitcast(I32))
+        def place_scales(plane, picked):
+            for q in range(QUADRANTS):
+                nc.sync.dma_start(plane[32 * q : 32 * q + 4, :].bitcast(I32), picked[ROW0 + 4 * q : ROW0 + 4 * q + 4, :].bitcast(I32))
 
+        nc.sync.dma_start(offs_sb[:], offs)
+        nc.sync.dma_start(xs[ROW0:, :].bitcast(I32), x_scales[0].bitcast(I32))
+        nc.sync.dma_start(w_raw[0][:], w_rows[:, :, W_CUTS[0] : W_CUTS[1]])
         nc.sync.dma_start(pro_sb[:], pro)
         nc.sync.dma_start(inv_row[P - 1 : P, :], inv[0:1, :])
-        nc.sync.dma_start(offs_sb[:], offs)
+        nc.sync.dma_start(es[ROW0:, :].bitcast(I32), e_scales[0].bitcast(I32))
+        nc.sync.dma_start(w_raw[1][:], w_rows[:, :, W_CUTS[1] : W_CUTS[2]])
         nc.sync.dma_start(xw[:].bitcast(I32), x_words[0].rearrange("p n t -> p (n t)").bitcast(I32))
-        load_scales(xs, x_scales, range(QUADRANTS - 1))
-        nc.sync.dma_start(w_raw[0][:], w_rows[:, :, 0 : H // 2])
-        load_scales(xs, x_scales, range(QUADRANTS - 1, QUADRANTS))
-        nc.sync.dma_start(w_raw[1][:], w_rows[:, :, H // 2 : H])
-        load_scales(es, e_scales, range(QUADRANTS))
-        nc.sync.dma_start(ew[:].bitcast(I32), e_words[0].rearrange("p n t -> p (n t)").bitcast(I32))
+        nc.sync.dma_start(w_raw[2][:], w_rows[:, :, W_CUTS[2] : W_CUTS[3]])
 
+        xsg = keep.tile([P, S], U8, name="xsg", align_bytes=64)
+        nc.vector.tensor_copy(xsg[:], xs[:].indirect(offs_sb[:]))
+        e_rows = e_words[0].rearrange("p n t -> p (n t)").bitcast(I32)
+        place_scales(x_plane, xsg)
+        nc.sync.dma_start(ew[:].bitcast(I32), e_rows)
         invg = keep.tile([P, V], F32, name="invg", align_bytes=64)
         nc.vector.tensor_copy(invg[:], inv_row[:].indirect(pro_sb[:]))
-        xsg = keep.tile([P, S], U8, name="xsg", align_bytes=64)
-        xwg = keep.tile([P, S], U32, name="xwg", tag="after_inv", align_bytes=64)
-        nc.vector.tensor_copy(xwg[:], xw[:].indirect(offs_sb[:]))
-        nc.vector.tensor_copy(xsg[:], xs[:].indirect(offs_sb[:]))
+        esg = keep.tile([P, V], U8, name="esg", align_bytes=64)
+        nc.vector.tensor_copy(esg[:], es[:].indirect(pro_sb[:]))
+        place_scales(e_plane, esg)
+        xwg = [keep.tile([P, S // 2], U32, name="xwg0", align_bytes=64)]
+        nc.vector.tensor_copy(xwg[0][:], xw[:].indirect(offs_sb[:, 0 : S // 32]))
 
         wg = keep.tile([P, PACK, P, PACK], BF16, name="wg", tag="after_wg", align_bytes=64)
-        shares = ((nc.scalar.copy, 0, 0, M_HALF), (nc.scalar.copy, 1, 0, M_SPLIT), (nc.vector.tensor_copy, 1, M_SPLIT, M_HALF))
-        for copy, u, lo, hi in shares:
-            copy(
-                wg[:, :, M_HALF * u + lo : M_HALF * u + hi, :].rearrange("p t m j -> p m t j"),
-                w_raw[u][:, :, PACK * lo : PACK * hi].rearrange("p j (m t) -> p m t j", t=PACK),
-            )
+        for u in range(3):
+            nc.scalar.copy(wg[:, :, W_CUTS[u] // PACK : W_CUTS[u + 1] // PACK, :].rearrange("p t m j -> p m t j"),
+                           w_raw[u][:].rearrange("p j (m t) -> p m t j", t=PACK))
         wc = keep.tile([P, H], U32, name="wc", align_bytes=64)
         ws = keep.tile([P, H], U8, name="ws", align_bytes=64)
         for u in range(2):
@@ -108,20 +114,20 @@ def tile_picked_yphi_log_p_kernel(tc, x_words, x_scales, w1, e_words, e_scales, 
             nc.vector.quantize_mx(out=wc[:, half].bitcast(FP8X4), scales=ws[:, half],
                                   in_=wg[:, 2 * u : 2 * u + 2].rearrange("p t m j -> p (t m j)"))
 
-        esg = keep.tile([P, V], U8, name="esg", tag="after_wg", align_bytes=64)
-        nc.vector.tensor_copy(esg[:], es[:].indirect(pro_sb[:]))
-        ewg = keep.tile([P, V], U32, name="ewg", tag="after_es", align_bytes=64)
+        xwg.append(keep.tile([P, S // 2], U32, name="xwg1", tag="after_wg", align_bytes=64))
+        nc.vector.tensor_copy(xwg[1][:], xw[:].indirect(offs_sb[:, S // 32 : S // 16]))
+        ewg = keep.tile([P, V], U32, name="ewg", tag="after_xw", align_bytes=64)
         nc.vector.tensor_copy(ewg[:], ew[:].indirect(pro_sb[:]))
 
         turned = psum.tile([P, V // P, P], F32, name="turned")
         for c in range(V // P):
             nc.tensor.transpose(turned[:, c, :], invg[:, c * P : (c + 1) * P], ident[:])
-        inv_col = keep.tile([P, V // P], F32, name="inv_col", align_bytes=64)
-        nc.vector.tensor_copy(inv_col[:], turned[:, :, P - 1])
+        inv_col = shared.tile([P, V // P], F32, name="inv_col", offset=0, align_bytes=64)
+        nc.scalar.copy(inv_col[:], turned[:, :, P - 1])
         spread = psum.tile([P, V], F32, name="spread")
         for c in range(V // P):
             nc.tensor.transpose(spread[:, c * P : (c + 1) * P], inv_col[:, c : c + 1].to_broadcast([P, P]), ident[:])
-        inv_all = shared.tile([P, V], F32, name="inv_all", offset=0, align_bytes=64)
+        inv_all = keep.tile([P, V], F32, name="inv_all", align_bytes=64)
         nc.scalar.copy(inv_all[:], spread[:])
 
         hc = keep.tile([P, S], U32, name="hc", align_bytes=64)
@@ -132,7 +138,7 @@ def tile_picked_yphi_log_p_kernel(tc, x_words, x_scales, w1, e_words, e_scales, 
             for t in range(PACK):
                 tcols = slice(t * P, (t + 1) * P)
                 nc.tensor.matmul_mx(out=hp[:, t, :], lhsT=wc[:, tcols].bitcast(FP8X4), lhsT_scale=ws[:, tcols],
-                                    rhs=xwg[:, cols].bitcast(FP8X4), rhs_scale=xsg[:, cols], start=True, stop=True)
+                                    rhs=xwg[b // 2][:, (b % 2) * P : (b % 2 + 1) * P].bitcast(FP8X4), rhs_scale=x_plane[:, cols], start=True, stop=True)
             hb = keep.tile([P, P, PACK], BF16, name=f"hb{b}", align_bytes=64)
             nc.scalar.copy(hb[:], hp[:].rearrange("p t n -> p n t"))
             nc.vector.quantize_mx(out=hc[:, cols].bitcast(FP8X4), scales=hs[:, cols], in_=hb[:].rearrange("p n t -> p (n t)"))
@@ -143,7 +149,7 @@ def tile_picked_yphi_log_p_kernel(tc, x_words, x_scales, w1, e_words, e_scales, 
             cols = slice(b * P, (b + 1) * P)
             yp = psum.tile([P, V], F32, name=f"yp{b}", tag="yp", bufs=2)
             nc.tensor.matmul_mx(out=yp[:], lhsT=hc[:, cols].bitcast(FP8X4), lhsT_scale=hs[:, cols],
-                                rhs=ewg[:].bitcast(FP8X4), rhs_scale=esg[:], start=True, stop=True)
+                                rhs=ewg[:].bitcast(FP8X4), rhs_scale=e_plane[:], start=True, stop=True)
             z = keep.tile([P, V], F32, name=f"z{b}", align_bytes=64)
             nc.vector.tensor_tensor(z[:], yp[:], inv_all[:], ALU.mult)
             neg_max = keep.tile([P, 1], F32, name=f"neg_max{b}")

@@ -28,7 +28,7 @@ LOG_ABOVE = 9
 NODES = LOG_BELOW + LOG_ABOVE + 1
 
 ROW0 = P - 16
-INV_SPLIT = 1408
+INV_SPLIT = 1280
 W_HALF_BYTES = PACK * (H // 2) * 4
 
 FLOPS = 2 * K * H * S + 2 * H * S * V
@@ -57,14 +57,16 @@ def tile_picked_yphi_log_p_kernel(tc, x_words, x_scales, w1, e_words, e_scales, 
         nodes_up = keep.tile([P, NODES], F32, name="nodes_up")
         ident = keep.tile([P, P], F32, name="ident", align_bytes=64)
 
+        zero = keep.tile([P, 1], F32, name="zero")
+        nc.gpsimd.memset(zero[:], 0.0)
         nc.gpsimd.memset(xs[0:ROW0, :].bitcast(I32), 0)
-        nc.gpsimd.memset(x_plane[:].bitcast(I32), 0)
-        nc.vector.memset(inv_row[0 : P - 1, 0:INV_SPLIT], 0.0)
         nc.gpsimd.iota(steps[:], [[1, NODES]], base=-LOG_BELOW, channel_multiplier=0, allow_small_or_imprecise_dtypes=True)
-        nc.gpsimd.memset(inv_row[0 : P - 1, INV_SPLIT:], 0.0)
-        nc.gpsimd.memset(es[0:ROW0, :].bitcast(I32), 0)
-        nc.gpsimd.memset(e_plane[:].bitcast(I32), 0)
         make_identity(nc, ident[:])
+        nc.vector.memset(x_plane[:].bitcast(I32), 0)
+        nc.vector.memset(inv_row[0 : P - 1, 0:INV_SPLIT], 0.0)
+        nc.vector.memset(es[0:ROW0, :].bitcast(I32), 0)
+        nc.vector.memset(e_plane[:].bitcast(I32), 0)
+        nc.scalar.copy(inv_row[0 : P - 1, INV_SPLIT:], zero[0 : P - 1, :].to_broadcast([P - 1, W - INV_SPLIT]))
 
         nc.scalar.activation(nodes_up[:], steps[:], ACT.Exp, scale=LOG_STEP)
         nc.scalar.mul(grid[:], nodes_up[:], -1.0)

@@ -20,7 +20,7 @@ PACK = 4
 QUADRANTS = 4
 K, T, S, H, V, W = 512, 1024, 512, 512, 512, 2048
 BLOCKS = S // P
-W_CUTS = (0, 3 * H // 8, 3 * H // 4, H)
+M_HALF = P // 2
 
 LOG_STEP = 0.375
 LOG_BELOW = 76
@@ -47,7 +47,7 @@ def tile_picked_yphi_log_p_kernel(tc, x_words, x_scales, w1, e_words, e_scales, 
 
         offs_sb = keep.tile([P, S // 16], U16, name="offs_sb")
         pro_sb = keep.tile([P, V // 16], U16, name="pro_sb")
-        xs = keep.tile([P, T], U8, name="xs", align_bytes=64)
+        xs = shared.tile([P, T], U8, name="xs", offset=W_HALF_BYTES, align_bytes=64)
         es = keep.tile([P, W], U8, name="es", align_bytes=64)
         inv_row = keep.tile([P, W], F32, name="inv_row", align_bytes=64)
         x_plane = keep.tile([P, S], U8, name="x_plane", align_bytes=64)
@@ -71,9 +71,8 @@ def tile_picked_yphi_log_p_kernel(tc, x_words, x_scales, w1, e_words, e_scales, 
         nc.scalar.activation(nodes_up[:], steps[:], ACT.Exp, scale=LOG_STEP)
         nc.scalar.mul(grid[:], nodes_up[:], -1.0)
 
-        w_raw = [shared.tile([P, PACK, W_CUTS[1]], F32, name="w_raw0", offset=W_HALF_BYTES, align_bytes=64),
-                 keep.tile([P, PACK, W_CUTS[2] - W_CUTS[1]], F32, name="w_raw1", align_bytes=64),
-                 shared.tile([P, PACK, H - W_CUTS[2]], F32, name="w_raw2", offset=0, align_bytes=64)]
+        w_raw = [keep.tile([P, PACK, H // 2], F32, name="w_raw0", align_bytes=64),
+                 shared.tile([P, PACK, H // 2], F32, name="w_raw1", offset=0, align_bytes=64)]
         xw = keep.tile([P, T], U32, name="xw", tag="after_xw", align_bytes=64)
         ew = shared.tile([P, W], U32, name="ew", offset=W_HALF_BYTES, align_bytes=64)
         w_rows = w1.rearrange("(p j) c -> p j c", j=PACK)
@@ -84,13 +83,12 @@ def tile_picked_yphi_log_p_kernel(tc, x_words, x_scales, w1, e_words, e_scales, 
 
         nc.sync.dma_start(offs_sb[:], offs)
         nc.sync.dma_start(xs[ROW0:, :].bitcast(I32), x_scales[0].bitcast(I32))
-        nc.sync.dma_start(w_raw[0][:], w_rows[:, :, W_CUTS[0] : W_CUTS[1]])
+        nc.sync.dma_start(w_raw[0][:], w_rows[:, :, 0 : H // 2])
         nc.sync.dma_start(pro_sb[:], pro)
         nc.sync.dma_start(inv_row[P - 1 : P, :], inv[0:1, :])
         nc.sync.dma_start(es[ROW0:, :].bitcast(I32), e_scales[0].bitcast(I32))
-        nc.sync.dma_start(w_raw[1][:], w_rows[:, :, W_CUTS[1] : W_CUTS[2]])
+        nc.sync.dma_start(w_raw[1][:], w_rows[:, :, H // 2 : H])
         nc.sync.dma_start(xw[:].bitcast(I32), x_words[0].rearrange("p n t -> p (n t)").bitcast(I32))
-        nc.sync.dma_start(w_raw[2][:], w_rows[:, :, W_CUTS[2] : W_CUTS[3]])
 
         xsg = keep.tile([P, S], U8, name="xsg", align_bytes=64)
         nc.vector.tensor_copy(xsg[:], xs[:].indirect(offs_sb[:]))
@@ -105,10 +103,10 @@ def tile_picked_yphi_log_p_kernel(tc, x_words, x_scales, w1, e_words, e_scales, 
         xwg = [keep.tile([P, S // 2], U32, name="xwg0", align_bytes=64)]
         nc.vector.tensor_copy(xwg[0][:], xw[:].indirect(offs_sb[:, 0 : S // 32]))
 
-        wg = keep.tile([P, PACK, P, PACK], BF16, name="wg", tag="after_wg", align_bytes=64)
-        for u in range(3):
-            nc.scalar.copy(wg[:, :, W_CUTS[u] // PACK : W_CUTS[u + 1] // PACK, :].rearrange("p t m j -> p m t j"),
-                           w_raw[u][:].rearrange("p j (m t) -> p m t j", t=PACK))
+        wg = keep.tile([P, PACK, P, PACK], BF16, name="wg", align_bytes=64)
+        for u in range(2):
+            nc.scalar.copy(wg[:, :, M_HALF * u : M_HALF * (u + 1), :].rearrange("p t m j -> p m j t"),
+                           w_raw[u][:].rearrange("p j (m t) -> p m j t", t=PACK))
         wc = keep.tile([P, H], U32, name="wc", align_bytes=64)
         ws = keep.tile([P, H], U8, name="ws", align_bytes=64)
         for u in range(2):
@@ -116,7 +114,7 @@ def tile_picked_yphi_log_p_kernel(tc, x_words, x_scales, w1, e_words, e_scales, 
             nc.vector.quantize_mx(out=wc[:, half].bitcast(FP8X4), scales=ws[:, half],
                                   in_=wg[:, 2 * u : 2 * u + 2].rearrange("p t m j -> p (t m j)"))
 
-        xwg.append(keep.tile([P, S // 2], U32, name="xwg1", tag="after_wg", align_bytes=64))
+        xwg.append(shared.tile([P, S // 2], U32, name="xwg1", offset=64, align_bytes=64))
         nc.vector.tensor_copy(xwg[1][:], xw[:].indirect(offs_sb[:, S // 32 : S // 16]))
         ewg = keep.tile([P, V], U32, name="ewg", tag="after_xw", align_bytes=64)
         nc.vector.tensor_copy(ewg[:], ew[:].indirect(pro_sb[:]))

@@ -28,7 +28,8 @@ LOG_ABOVE = 9
 NODES = LOG_BELOW + LOG_ABOVE + 1
 
 ROW0 = P - 16
-INV_SPLIT = 1280
+INV_SPLIT = 1664
+X_PIECES = ((0, 1), (1, 2), (2, 4))
 W_HALF_BYTES = PACK * (H // 2) * 4
 
 FLOPS = 2 * K * H * S + 2 * H * S * V
@@ -47,34 +48,19 @@ def tile_picked_yphi_log_p_kernel(tc, x_words, x_scales, w1, e_words, e_scales, 
 
         offs_sb = keep.tile([P, S // 16], U16, name="offs_sb")
         pro_sb = keep.tile([P, V // 16], U16, name="pro_sb")
-        xs = shared.tile([P, T], U8, name="xs", offset=W_HALF_BYTES, align_bytes=64)
-        es = keep.tile([P, W], U8, name="es", align_bytes=64)
-        inv_row = keep.tile([P, W], F32, name="inv_row", align_bytes=64)
+        xs = keep.tile([P, T], U8, name="xs", align_bytes=64)
+        es = keep.tile([P, W], U8, name="es", tag="after_es", align_bytes=64)
+        inv_row = shared.tile([P, W], F32, name="inv_row", offset=W_HALF_BYTES, align_bytes=64)
         x_plane = keep.tile([P, S], U8, name="x_plane", align_bytes=64)
-        e_plane = keep.tile([P, V], U8, name="e_plane", align_bytes=64)
         steps = keep.tile([P, NODES], F32, name="steps")
         grid = keep.tile([P, NODES], F32, name="grid")
         nodes_up = keep.tile([P, NODES], F32, name="nodes_up")
         ident = keep.tile([P, P], F32, name="ident", align_bytes=64)
 
-        zero = keep.tile([P, 1], F32, name="zero")
-        nc.gpsimd.memset(zero[:], 0.0)
-        nc.gpsimd.memset(xs[0:ROW0, :].bitcast(I32), 0)
-        nc.gpsimd.iota(steps[:], [[1, NODES]], base=-LOG_BELOW, channel_multiplier=0, allow_small_or_imprecise_dtypes=True)
-        make_identity(nc, ident[:])
-        nc.vector.memset(x_plane[:].bitcast(I32), 0)
-        nc.vector.memset(inv_row[0 : P - 1, 0:INV_SPLIT], 0.0)
-        nc.vector.memset(es[0:ROW0, :].bitcast(I32), 0)
-        nc.vector.memset(e_plane[:].bitcast(I32), 0)
-        nc.scalar.copy(inv_row[0 : P - 1, INV_SPLIT:], zero[0 : P - 1, :].to_broadcast([P - 1, W - INV_SPLIT]))
-
-        nc.scalar.activation(nodes_up[:], steps[:], ACT.Exp, scale=LOG_STEP)
-        nc.scalar.mul(grid[:], nodes_up[:], -1.0)
-
         w_raw = [keep.tile([P, PACK, H // 2], F32, name="w_raw0", align_bytes=64),
                  shared.tile([P, PACK, H // 2], F32, name="w_raw1", offset=0, align_bytes=64)]
-        xw = keep.tile([P, T], U32, name="xw", tag="after_xw", align_bytes=64)
-        ew = shared.tile([P, W], U32, name="ew", offset=W_HALF_BYTES, align_bytes=64)
+        xw = keep.tile([P, T], U32, name="xw", align_bytes=64)
+        ew = shared.tile([P, W], U32, name="ew", offset=W_HALF_BYTES + V + 2 * PACK * H, align_bytes=64)
         w_rows = w1.rearrange("(p j) c -> p j c", j=PACK)
 
         def place_scales(plane, picked):
@@ -83,12 +69,24 @@ def tile_picked_yphi_log_p_kernel(tc, x_words, x_scales, w1, e_words, e_scales, 
 
         nc.sync.dma_start(offs_sb[:], offs)
         nc.sync.dma_start(xs[ROW0:, :].bitcast(I32), x_scales[0].bitcast(I32))
-        nc.sync.dma_start(w_raw[0][:], w_rows[:, :, 0 : H // 2])
         nc.sync.dma_start(pro_sb[:], pro)
         nc.sync.dma_start(inv_row[P - 1 : P, :], inv[0:1, :])
+        nc.sync.dma_start(w_raw[0][:], w_rows[:, :, 0 : H // 2])
         nc.sync.dma_start(es[ROW0:, :].bitcast(I32), e_scales[0].bitcast(I32))
         nc.sync.dma_start(w_raw[1][:], w_rows[:, :, H // 2 : H])
         nc.sync.dma_start(xw[:].bitcast(I32), x_words[0].rearrange("p n t -> p (n t)").bitcast(I32))
+
+        zero = keep.tile([P, 1], F32, name="zero")
+        nc.gpsimd.memset(zero[:], 0.0)
+        nc.gpsimd.memset(xs[0:ROW0, :].bitcast(I32), 0)
+        nc.gpsimd.memset(es[0:ROW0, :].bitcast(I32), 0)
+        nc.gpsimd.iota(steps[:], [[1, NODES]], base=-LOG_BELOW, channel_multiplier=0, allow_small_or_imprecise_dtypes=True)
+        make_identity(nc, ident[:])
+        nc.vector.memset(x_plane[:].bitcast(I32), 0)
+        nc.vector.memset(inv_row[0 : P - 1, 0:INV_SPLIT], 0.0)
+
+        nc.scalar.activation(nodes_up[:], steps[:], ACT.Exp, scale=LOG_STEP)
+        nc.scalar.copy(inv_row[0 : P - 1, INV_SPLIT:], zero[0 : P - 1, :].to_broadcast([P - 1, W - INV_SPLIT]))
 
         xsg = keep.tile([P, S], U8, name="xsg", align_bytes=64)
         nc.vector.tensor_copy(xsg[:], xs[:].indirect(offs_sb[:]))
@@ -96,17 +94,19 @@ def tile_picked_yphi_log_p_kernel(tc, x_words, x_scales, w1, e_words, e_scales, 
         place_scales(x_plane, xsg)
         nc.sync.dma_start(ew[:].bitcast(I32), e_rows)
         invg = keep.tile([P, V], F32, name="invg", align_bytes=64)
-        nc.vector.tensor_copy(invg[:], inv_row[:].indirect(pro_sb[:]))
+        nc.scalar.activation(invg[:], inv_row[:].indirect(pro_sb[:]), ACT.Copy)
         esg = keep.tile([P, V], U8, name="esg", align_bytes=64)
         nc.vector.tensor_copy(esg[:], es[:].indirect(pro_sb[:]))
+        e_plane = shared.tile([P, V], U8, name="e_plane", offset=W_HALF_BYTES, align_bytes=64)
+        nc.gpsimd.memset(e_plane[:].bitcast(I32), 0)
         place_scales(e_plane, esg)
-        xwg = [keep.tile([P, S // 2], U32, name="xwg0", align_bytes=64)]
-        nc.vector.tensor_copy(xwg[0][:], xw[:].indirect(offs_sb[:, 0 : S // 32]))
+
+        nc.gpsimd.tensor_scalar(grid[:], nodes_up[:], -1.0, 0.0, ALU.mult, ALU.add)
 
         wg = keep.tile([P, PACK, P, PACK], BF16, name="wg", align_bytes=64)
-        for u in range(2):
-            nc.scalar.copy(wg[:, :, M_HALF * u : M_HALF * (u + 1), :].rearrange("p t m j -> p m j t"),
-                           w_raw[u][:].rearrange("p j (m t) -> p m j t", t=PACK))
+        for u, copy in enumerate((nc.vector.tensor_copy, nc.scalar.copy)):
+            copy(wg[:, :, M_HALF * u : M_HALF * (u + 1), :].rearrange("p t m j -> p m j t"),
+                 w_raw[u][:].rearrange("p j (m t) -> p m j t", t=PACK))
         wc = keep.tile([P, H], U32, name="wc", align_bytes=64)
         ws = keep.tile([P, H], U8, name="ws", align_bytes=64)
         for u in range(2):
@@ -114,15 +114,19 @@ def tile_picked_yphi_log_p_kernel(tc, x_words, x_scales, w1, e_words, e_scales, 
             nc.vector.quantize_mx(out=wc[:, half].bitcast(FP8X4), scales=ws[:, half],
                                   in_=wg[:, 2 * u : 2 * u + 2].rearrange("p t m j -> p (t m j)"))
 
-        xwg.append(shared.tile([P, S // 2], U32, name="xwg1", offset=64, align_bytes=64))
-        nc.vector.tensor_copy(xwg[1][:], xw[:].indirect(offs_sb[:, S // 32 : S // 16]))
-        ewg = keep.tile([P, V], U32, name="ewg", tag="after_xw", align_bytes=64)
-        nc.vector.tensor_copy(ewg[:], ew[:].indirect(pro_sb[:]))
+        xwg = []
+        for b0, b1 in X_PIECES:
+            if b0 == 0:
+                piece = keep.tile([P, (b1 - b0) * P], U32, name="xwg0", tag="after_es", align_bytes=64)
+            else:
+                piece = shared.tile([P, (b1 - b0) * P], U32, name=f"xwg{b0}", offset=4 * P * b0, align_bytes=64)
+            nc.vector.tensor_copy(piece[:], xw[:].indirect(offs_sb[:, b0 * P // 16 : b1 * P // 16]))
+            xwg.extend(piece[:, (b - b0) * P : (b - b0 + 1) * P] for b in range(b0, b1))
 
         turned = psum.tile([P, V // P, P], F32, name="turned")
         for c in range(V // P):
             nc.tensor.transpose(turned[:, c, :], invg[:, c * P : (c + 1) * P], ident[:])
-        inv_col = shared.tile([P, V // P], F32, name="inv_col", offset=0, align_bytes=64)
+        inv_col = keep.tile([P, V // P], F32, name="inv_col", align_bytes=64)
         nc.scalar.copy(inv_col[:], turned[:, :, P - 1])
         spread = psum.tile([P, V], F32, name="spread")
         for c in range(V // P):
@@ -131,24 +135,29 @@ def tile_picked_yphi_log_p_kernel(tc, x_words, x_scales, w1, e_words, e_scales, 
         nc.scalar.copy(inv_all[:], spread[:])
 
         hc = keep.tile([P, S], U32, name="hc", align_bytes=64)
-        hs = shared.tile([P, S], U8, name="hs", offset=W_HALF_BYTES, align_bytes=64)
+        hs0 = keep.tile([P, P], U8, name="hs0", align_bytes=64)
+        hs_late = shared.tile([P, S - P], U8, name="hs_late", offset=W_HALF_BYTES + V + 2 * PACK * H, align_bytes=64)
+        hs = [hs0[:]] + [hs_late[:, b * P : (b + 1) * P] for b in range(BLOCKS - 1)]
+        ewg = keep.tile([P, V], U32, name="ewg", align_bytes=64)
         for b in range(BLOCKS):
             cols = slice(b * P, (b + 1) * P)
             hp = psum.tile([P, PACK, P], F32, name=f"hp{b}", tag="acc", bufs=BLOCKS)
             for t in range(PACK):
                 tcols = slice(t * P, (t + 1) * P)
                 nc.tensor.matmul_mx(out=hp[:, t, :], lhsT=wc[:, tcols].bitcast(FP8X4), lhsT_scale=ws[:, tcols],
-                                    rhs=xwg[b // 2][:, (b % 2) * P : (b % 2 + 1) * P].bitcast(FP8X4), rhs_scale=x_plane[:, cols], start=True, stop=True)
+                                    rhs=xwg[b].bitcast(FP8X4), rhs_scale=x_plane[:, cols], start=True, stop=True)
             hb = keep.tile([P, P, PACK], BF16, name=f"hb{b}", align_bytes=64)
             nc.scalar.copy(hb[:], hp[:].rearrange("p t n -> p n t"))
-            nc.vector.quantize_mx(out=hc[:, cols].bitcast(FP8X4), scales=hs[:, cols], in_=hb[:].rearrange("p n t -> p (n t)"))
+            nc.vector.quantize_mx(out=hc[:, cols].bitcast(FP8X4), scales=hs[b], in_=hb[:].rearrange("p n t -> p (n t)"))
+            if b == 0:
+                nc.vector.tensor_copy(ewg[:], ew[:].indirect(pro_sb[:]))
 
         rows = []
         scratch = [keep.tile([P, V], F32, name="scratch0", align_bytes=64)]
         for b in range(BLOCKS):
             cols = slice(b * P, (b + 1) * P)
             yp = psum.tile([P, V], F32, name=f"yp{b}", tag="yp", bufs=2)
-            nc.tensor.matmul_mx(out=yp[:], lhsT=hc[:, cols].bitcast(FP8X4), lhsT_scale=hs[:, cols],
+            nc.tensor.matmul_mx(out=yp[:], lhsT=hc[:, cols].bitcast(FP8X4), lhsT_scale=hs[b],
                                 rhs=ewg[:].bitcast(FP8X4), rhs_scale=e_plane[:], start=True, stop=True)
             z = keep.tile([P, V], F32, name=f"z{b}", align_bytes=64)
             nc.vector.tensor_tensor(z[:], yp[:], inv_all[:], ALU.mult)

@@ -20,7 +20,6 @@ PACK = 4
 QUADRANTS = 4
 K, T, S, H, V, W = 512, 1024, 512, 512, 512, 2048
 BLOCKS = S // P
-M_HALF = P // 2
 
 LOG_STEP = 0.375
 LOG_BELOW = 76
@@ -28,9 +27,9 @@ LOG_ABOVE = 9
 NODES = LOG_BELOW + LOG_ABOVE + 1
 
 ROW0 = P - 16
-INV_SPLIT = 1664
+INV_SPLIT = 1280
 X_PIECES = ((0, 1), (1, 2), (2, 4))
-W_HALF_BYTES = PACK * (H // 2) * 4
+W_BYTES = PACK * H * 4
 
 FLOPS = 2 * K * H * S + 2 * H * S * V
 BYTES = K * T + K * T // 32 + 4 * K * H + H * W + H * W // 32 + 4 * W + 2 * P * (S + V) // 16 + 4 * S * V
@@ -48,20 +47,19 @@ def tile_picked_yphi_log_p_kernel(tc, x_words, x_scales, w1, e_words, e_scales, 
 
         offs_sb = keep.tile([P, S // 16], U16, name="offs_sb")
         pro_sb = keep.tile([P, V // 16], U16, name="pro_sb")
-        xs = keep.tile([P, T], U8, name="xs", align_bytes=64)
+        xs = shared.tile([P, T], U8, name="xs", offset=W_BYTES, align_bytes=64)
         es = keep.tile([P, W], U8, name="es", tag="after_es", align_bytes=64)
-        inv_row = shared.tile([P, W], F32, name="inv_row", offset=W_HALF_BYTES, align_bytes=64)
+        inv_row = keep.tile([P, W], F32, name="inv_row", align_bytes=64)
         x_plane = keep.tile([P, S], U8, name="x_plane", align_bytes=64)
+        e_plane = keep.tile([P, V], U8, name="e_plane", align_bytes=64)
         steps = keep.tile([P, NODES], F32, name="steps")
         grid = keep.tile([P, NODES], F32, name="grid")
         nodes_up = keep.tile([P, NODES], F32, name="nodes_up")
         ident = keep.tile([P, P], F32, name="ident", align_bytes=64)
 
-        w_raw = [keep.tile([P, PACK, H // 2], F32, name="w_raw0", align_bytes=64),
-                 shared.tile([P, PACK, H // 2], F32, name="w_raw1", offset=0, align_bytes=64)]
+        w_raw = shared.tile([P, PACK, H], F32, name="w_raw", offset=0, align_bytes=64)
         xw = keep.tile([P, T], U32, name="xw", align_bytes=64)
-        ew = shared.tile([P, W], U32, name="ew", offset=W_HALF_BYTES + V + 2 * PACK * H, align_bytes=64)
-        w_rows = w1.rearrange("(p j) c -> p j c", j=PACK)
+        ew = shared.tile([P, W], U32, name="ew", offset=W_BYTES, align_bytes=64)
 
         def place_scales(plane, picked):
             for q in range(QUADRANTS):
@@ -71,19 +69,19 @@ def tile_picked_yphi_log_p_kernel(tc, x_words, x_scales, w1, e_words, e_scales, 
         nc.sync.dma_start(xs[ROW0:, :].bitcast(I32), x_scales[0].bitcast(I32))
         nc.sync.dma_start(pro_sb[:], pro)
         nc.sync.dma_start(inv_row[P - 1 : P, :], inv[0:1, :])
-        nc.sync.dma_start(w_raw[0][:], w_rows[:, :, 0 : H // 2])
         nc.sync.dma_start(es[ROW0:, :].bitcast(I32), e_scales[0].bitcast(I32))
-        nc.sync.dma_start(w_raw[1][:], w_rows[:, :, H // 2 : H])
+        nc.sync.dma_start(w_raw[:], w1.rearrange("(p j) c -> p j c", j=PACK))
         nc.sync.dma_start(xw[:].bitcast(I32), x_words[0].rearrange("p n t -> p (n t)").bitcast(I32))
 
         zero = keep.tile([P, 1], F32, name="zero")
         nc.gpsimd.memset(zero[:], 0.0)
         nc.gpsimd.memset(xs[0:ROW0, :].bitcast(I32), 0)
-        nc.gpsimd.memset(es[0:ROW0, :].bitcast(I32), 0)
         nc.gpsimd.iota(steps[:], [[1, NODES]], base=-LOG_BELOW, channel_multiplier=0, allow_small_or_imprecise_dtypes=True)
         make_identity(nc, ident[:])
         nc.vector.memset(x_plane[:].bitcast(I32), 0)
         nc.vector.memset(inv_row[0 : P - 1, 0:INV_SPLIT], 0.0)
+        nc.vector.memset(es[0:ROW0, :].bitcast(I32), 0)
+        nc.vector.memset(e_plane[:].bitcast(I32), 0)
 
         nc.scalar.activation(nodes_up[:], steps[:], ACT.Exp, scale=LOG_STEP)
         nc.scalar.copy(inv_row[0 : P - 1, INV_SPLIT:], zero[0 : P - 1, :].to_broadcast([P - 1, W - INV_SPLIT]))
@@ -97,31 +95,34 @@ def tile_picked_yphi_log_p_kernel(tc, x_words, x_scales, w1, e_words, e_scales, 
         nc.scalar.activation(invg[:], inv_row[:].indirect(pro_sb[:]), ACT.Copy)
         esg = keep.tile([P, V], U8, name="esg", align_bytes=64)
         nc.vector.tensor_copy(esg[:], es[:].indirect(pro_sb[:]))
-        e_plane = shared.tile([P, V], U8, name="e_plane", offset=W_HALF_BYTES, align_bytes=64)
-        nc.gpsimd.memset(e_plane[:].bitcast(I32), 0)
         place_scales(e_plane, esg)
 
-        nc.gpsimd.tensor_scalar(grid[:], nodes_up[:], -1.0, 0.0, ALU.mult, ALU.add)
+        nc.scalar.mul(grid[:], nodes_up[:], -1.0)
 
-        wg = keep.tile([P, PACK, P, PACK], BF16, name="wg", align_bytes=64)
-        for u, copy in enumerate((nc.vector.tensor_copy, nc.scalar.copy)):
-            copy(wg[:, :, M_HALF * u : M_HALF * (u + 1), :].rearrange("p t m j -> p m j t"),
-                 w_raw[u][:].rearrange("p j (m t) -> p m j t", t=PACK))
-        wc = keep.tile([P, H], U32, name="wc", align_bytes=64)
-        ws = keep.tile([P, H], U8, name="ws", align_bytes=64)
-        for u in range(2):
-            half = slice(u * H // 2, (u + 1) * H // 2)
-            nc.vector.quantize_mx(out=wc[:, half].bitcast(FP8X4), scales=ws[:, half],
-                                  in_=wg[:, 2 * u : 2 * u + 2].rearrange("p t m j -> p (t m j)"))
-
+        wg = [keep.tile([P, 2, P, PACK], BF16, name=f"wg{pair}", align_bytes=64) for pair in range(2)]
+        for pair, copy in enumerate((nc.vector.tensor_copy, nc.scalar.copy)):
+            copy(wg[pair][:].rearrange("p t m j -> p m j t"),
+                 w_raw[:].rearrange("p j (m t) -> p m j t", t=PACK)[:, :, :, 2 * pair : 2 * pair + 2])
         xwg = []
-        for b0, b1 in X_PIECES:
+
+        def gather_x(b0, b1):
             if b0 == 0:
                 piece = keep.tile([P, (b1 - b0) * P], U32, name="xwg0", tag="after_es", align_bytes=64)
             else:
                 piece = shared.tile([P, (b1 - b0) * P], U32, name=f"xwg{b0}", offset=4 * P * b0, align_bytes=64)
             nc.vector.tensor_copy(piece[:], xw[:].indirect(offs_sb[:, b0 * P // 16 : b1 * P // 16]))
             xwg.extend(piece[:, (b - b0) * P : (b - b0 + 1) * P] for b in range(b0, b1))
+
+        gather_x(*X_PIECES[0])
+        wc = keep.tile([P, H], U32, name="wc", align_bytes=64)
+        ws = keep.tile([P, H], U8, name="ws", align_bytes=64)
+        for u in range(2):
+            half = slice(u * H // 2, (u + 1) * H // 2)
+            nc.vector.quantize_mx(out=wc[:, half].bitcast(FP8X4), scales=ws[:, half],
+                                  in_=wg[u][:].rearrange("p t m j -> p (t m j)"))
+
+        for piece in X_PIECES[1:]:
+            gather_x(*piece)
 
         turned = psum.tile([P, V // P, P], F32, name="turned")
         for c in range(V // P):
@@ -136,7 +137,7 @@ def tile_picked_yphi_log_p_kernel(tc, x_words, x_scales, w1, e_words, e_scales, 
 
         hc = keep.tile([P, S], U32, name="hc", align_bytes=64)
         hs0 = keep.tile([P, P], U8, name="hs0", align_bytes=64)
-        hs_late = shared.tile([P, S - P], U8, name="hs_late", offset=W_HALF_BYTES + V + 2 * PACK * H, align_bytes=64)
+        hs_late = shared.tile([P, S - P], U8, name="hs_late", offset=W_BYTES, align_bytes=64)
         hs = [hs0[:]] + [hs_late[:, b * P : (b + 1) * P] for b in range(BLOCKS - 1)]
         ewg = keep.tile([P, V], U32, name="ewg", align_bytes=64)
         for b in range(BLOCKS):

@@ -30,6 +30,7 @@ ROW0 = P - 16
 INV_SPLIT = 1280
 X_PIECES = ((0, 1), (1, 2), (2, 4))
 W_BYTES = PACK * H * 4
+E_SCALES_AT = W_BYTES + 4 * W
 
 FLOPS = 2 * K * H * S + 2 * H * S * V
 BYTES = K * T + K * T // 32 + 4 * K * H + H * W + H * W // 32 + 4 * W + 2 * P * (S + V) // 16 + 4 * S * V
@@ -48,7 +49,7 @@ def tile_picked_yphi_log_p_kernel(tc, x_words, x_scales, w1, e_words, e_scales, 
         offs_sb = keep.tile([P, S // 16], U16, name="offs_sb")
         pro_sb = keep.tile([P, V // 16], U16, name="pro_sb")
         xs = shared.tile([P, T], U8, name="xs", offset=W_BYTES, align_bytes=64)
-        es = keep.tile([P, W], U8, name="es", tag="after_es", align_bytes=64)
+        es = shared.tile([P, W], U8, name="es", offset=E_SCALES_AT, align_bytes=64)
         inv_row = keep.tile([P, W], F32, name="inv_row", align_bytes=64)
         x_plane = keep.tile([P, S], U8, name="x_plane", align_bytes=64)
         e_plane = keep.tile([P, V], U8, name="e_plane", align_bytes=64)
@@ -107,7 +108,7 @@ def tile_picked_yphi_log_p_kernel(tc, x_words, x_scales, w1, e_words, e_scales, 
 
         def gather_x(b0, b1):
             if b0 == 0:
-                piece = keep.tile([P, (b1 - b0) * P], U32, name="xwg0", tag="after_es", align_bytes=64)
+                piece = shared.tile([P, (b1 - b0) * P], U32, name="xwg0", offset=E_SCALES_AT, align_bytes=64)
             else:
                 piece = shared.tile([P, (b1 - b0) * P], U32, name=f"xwg{b0}", offset=4 * P * b0, align_bytes=64)
             nc.vector.tensor_copy(piece[:], xw[:].indirect(offs_sb[:, b0 * P // 16 : b1 * P // 16]))
@@ -127,8 +128,8 @@ def tile_picked_yphi_log_p_kernel(tc, x_words, x_scales, w1, e_words, e_scales, 
         turned = psum.tile([P, V // P, P], F32, name="turned")
         for c in range(V // P):
             nc.tensor.transpose(turned[:, c, :], invg[:, c * P : (c + 1) * P], ident[:])
-        inv_col = keep.tile([P, V // P], F32, name="inv_col", align_bytes=64)
-        nc.scalar.copy(inv_col[:], turned[:, :, P - 1])
+        inv_col = shared.tile([P, V // P], F32, name="inv_col", offset=E_SCALES_AT + 4 * P, align_bytes=64)
+        nc.vector.tensor_copy(inv_col[:], turned[:, :, P - 1])
         spread = psum.tile([P, V], F32, name="spread")
         for c in range(V // P):
             nc.tensor.transpose(spread[:, c * P : (c + 1) * P], inv_col[:, c : c + 1].to_broadcast([P, P]), ident[:])

@@ -154,34 +154,56 @@ def tile_picked_yphi_log_p_kernel(tc, x_words, x_scales, w1, e_words, e_scales, 
             if b == 0:
                 nc.vector.tensor_copy(ewg[:], ew[:].indirect(pro_sb[:]))
 
-        rows = []
-        scratch = [keep.tile([P, V], F32, name="scratch0", align_bytes=64)]
-        for b in range(BLOCKS):
+        z, neg_max, total, rest, base = {}, {}, {}, {}, {}
+
+        def scale(b):
             cols = slice(b * P, (b + 1) * P)
             yp = psum.tile([P, V], F32, name=f"yp{b}", tag="yp", bufs=2)
             nc.tensor.matmul_mx(out=yp[:], lhsT=hc[:, cols].bitcast(FP8X4), lhsT_scale=hs[b],
                                 rhs=ewg[:].bitcast(FP8X4), rhs_scale=e_plane[:], start=True, stop=True)
-            z = keep.tile([P, V], F32, name=f"z{b}", align_bytes=64)
-            nc.vector.tensor_tensor(z[:], yp[:], inv_all[:], ALU.mult)
-            neg_max = keep.tile([P, 1], F32, name=f"neg_max{b}")
-            nc.vector.tensor_reduce(neg_max[:], z[:], AXIS.X, ALU.max, negate=True)
-            total = keep.tile([P, 1], F32, name=f"total{b}")
-            nc.scalar.activation(scratch[b % 2][:], z[:], ACT.Exp, bias=neg_max[:], accum_out=total[:])
-            base = keep.tile([P, 1], F32, name=f"base{b}")
-            nc.scalar.activation(base[:], neg_max[:], ACT.Identity, bias=-sum_at_one)
-            rest = keep.tile([P, 1], F32, name=f"rest{b}", tag="after_rest0" if b == 0 else f"rest{b}", align_bytes=64)
-            nc.scalar.activation(scratch[b % 2][:, 0:NODES], grid[:], ACT.Exp, bias=log_of_step, scale=total[:], accum_out=rest[:])
-            rows.append((z, base, rest))
-            if b == 0:
-                shift = keep.tile([P, 1], F32, name="shift")
-                nc.scalar.activation(shift[:], rest[:], ACT.Identity, bias=base[:])
-                first = keep.tile([P, V], F32, name="res0", align_bytes=64)
-                nc.gpsimd.tensor_scalar(first[:], z[:], shift[:], 1.0, ALU.add, ALU.mult)
-                nc.sync.dma_start(out[cols, :], first[:])
-                scratch.append(keep.tile([P, V], F32, name="scratch1", tag="after_rest0", align_bytes=64))
+            z[b] = keep.tile([P, V], F32, name=f"z{b}", align_bytes=64)
+            nc.vector.tensor_tensor(z[b][:], yp[:], inv_all[:], ALU.mult)
 
-        for b in range(1, BLOCKS):
-            z, base, rest = rows[b]
+        def row_max(b):
+            neg_max[b] = keep.tile([P, 1], F32, name=f"neg_max{b}")
+            nc.vector.tensor_reduce(neg_max[b][:], z[b][:], AXIS.X, ALU.max, negate=True)
+
+        def row_sum(b):
+            total[b] = keep.tile([P, 1], F32, name=f"total{b}")
+            terms = keep.tile([P, V], F32, name=f"terms{b}", align_bytes=64)
+            nc.scalar.activation(terms[:], z[b][:], ACT.Exp, bias=neg_max[b][:], accum_out=total[b][:])
+            base[b] = keep.tile([P, 1], F32, name=f"base{b}")
+            nc.scalar.activation(base[b][:], neg_max[b][:], ACT.Identity, bias=-sum_at_one)
+
+        def row_log(b):
+            rest[b] = keep.tile([P, 1], F32, name=f"rest{b}")
+            terms = keep.tile([P, NODES], F32, name=f"log_terms{b}", align_bytes=64)
+            nc.scalar.activation(terms[:], grid[:], ACT.Exp, bias=log_of_step, scale=total[b][:], accum_out=rest[b][:])
+
+        def finish(b, pieces):
             res = keep.tile([P, V], F32, name=f"res{b}", align_bytes=64)
-            nc.vector.tensor_scalar(res[:], z[:], base[:], rest[:], ALU.add, ALU.add)
-            nc.sync.dma_start(out[b * P : (b + 1) * P, :], res[:])
+            for c0 in range(0, V, V // pieces):
+                cols = slice(c0, c0 + V // pieces)
+                nc.vector.tensor_scalar(res[:, cols], z[b][:, cols], base[b][:], rest[b][:], ALU.add, ALU.add)
+                nc.sync.dma_start(out[b * P : (b + 1) * P, cols], res[:, cols])
+
+        scale(0)
+        scale(1)
+        row_max(0)
+        row_sum(0)
+        row_log(0)
+        scale(2)
+        row_max(1)
+        row_sum(1)
+        row_max(2)
+        row_sum(2)
+        row_log(1)
+        row_log(2)
+        scale(3)
+        finish(0, 1)
+        row_max(3)
+        row_sum(3)
+        row_log(3)
+        finish(1, 1)
+        finish(2, 1)
+        finish(3, 2)

@@ -27,7 +27,7 @@ LOG_ABOVE = 9
 NODES = LOG_BELOW + LOG_ABOVE + 1
 
 ROW0 = P - 16
-INV_SPLIT = 1280
+INV_SPLIT = 1536
 X_PIECES = ((0, 1), (1, 2), (2, 4))
 W_BYTES = PACK * H * 4
 E_SCALES_AT = W_BYTES + 4 * W
@@ -79,13 +79,11 @@ def tile_picked_yphi_log_p_kernel(tc, x_words, x_scales, w1, e_words, e_scales, 
         nc.gpsimd.memset(xs[0:ROW0, :].bitcast(I32), 0)
         nc.gpsimd.iota(steps[:], [[1, NODES]], base=-LOG_BELOW, channel_multiplier=0, allow_small_or_imprecise_dtypes=True)
         make_identity(nc, ident[:])
-        nc.vector.memset(x_plane[:].bitcast(I32), 0)
         nc.vector.memset(inv_row[0 : P - 1, 0:INV_SPLIT], 0.0)
         nc.vector.memset(es[0:ROW0, :].bitcast(I32), 0)
-        nc.vector.memset(e_plane[:].bitcast(I32), 0)
 
         nc.scalar.activation(nodes_up[:], steps[:], ACT.Exp, scale=LOG_STEP)
-        nc.scalar.copy(inv_row[0 : P - 1, INV_SPLIT:], zero[0 : P - 1, :].to_broadcast([P - 1, W - INV_SPLIT]))
+        nc.scalar.activation(inv_row[0 : P - 1, INV_SPLIT:], zero[0 : P - 1, :].to_broadcast([P - 1, W - INV_SPLIT]), ACT.Copy)
 
         xsg = keep.tile([P, S], U8, name="xsg", align_bytes=64)
         nc.vector.tensor_copy(xsg[:], xs[:].indirect(offs_sb[:]))

@@ -31,6 +31,7 @@ INV_SPLIT = 1536
 X_PIECES = ((0, 1), (1, 2), (2, 4))
 W_BYTES = PACK * H * 4
 E_SCALES_AT = W_BYTES + 4 * W
+PICKED_ES_AT = E_SCALES_AT + W + S
 
 FLOPS = 2 * K * H * S + 2 * H * S * V
 BYTES = K * T + K * T // 32 + 4 * K * H + H * W + H * W // 32 + 4 * W + 2 * P * (S + V) // 16 + 4 * S * V
@@ -92,7 +93,7 @@ def tile_picked_yphi_log_p_kernel(tc, x_words, x_scales, w1, e_words, e_scales, 
         nc.sync.dma_start(ew[:].bitcast(I32), e_rows)
         invg = keep.tile([P, V], F32, name="invg", align_bytes=64)
         nc.scalar.activation(invg[:], inv_row[:].indirect(pro_sb[:]), ACT.Copy)
-        esg = keep.tile([P, V], U8, name="esg", align_bytes=64)
+        esg = shared.tile([P, V], U8, name="esg", offset=PICKED_ES_AT, align_bytes=64)
         nc.vector.tensor_copy(esg[:], es[:].indirect(pro_sb[:]))
         place_scales(e_plane, esg)
 
@@ -123,42 +124,49 @@ def tile_picked_yphi_log_p_kernel(tc, x_words, x_scales, w1, e_words, e_scales, 
         for piece in X_PIECES[1:]:
             gather_x(*piece)
 
-        turned = psum.tile([P, V // P, P], F32, name="turned")
+        turned = psum.tile([P, V // P, P], F32, name="turned", tag="turned")
         for c in range(V // P):
             nc.tensor.transpose(turned[:, c, :], invg[:, c * P : (c + 1) * P], ident[:])
         inv_col = shared.tile([P, V // P], F32, name="inv_col", offset=E_SCALES_AT + 4 * P, align_bytes=64)
         nc.vector.tensor_copy(inv_col[:], turned[:, :, P - 1])
-        spread = psum.tile([P, V], F32, name="spread")
+        spread = psum.tile([P, V], F32, name="spread", tag="spread")
         for c in range(V // P):
             nc.tensor.transpose(spread[:, c * P : (c + 1) * P], inv_col[:, c : c + 1].to_broadcast([P, P]), ident[:])
         inv_all = keep.tile([P, V], F32, name="inv_all", align_bytes=64)
         nc.scalar.copy(inv_all[:], spread[:])
 
         hc = keep.tile([P, S], U32, name="hc", align_bytes=64)
-        hs0 = keep.tile([P, P], U8, name="hs0", align_bytes=64)
-        hs_late = shared.tile([P, S - P], U8, name="hs_late", offset=W_BYTES, align_bytes=64)
-        hs = [hs0[:]] + [hs_late[:, b * P : (b + 1) * P] for b in range(BLOCKS - 1)]
-        ewg = keep.tile([P, V], U32, name="ewg", align_bytes=64)
+        hs_all = shared.tile([P, S], U8, name="hs_all", offset=PICKED_ES_AT + 64 - S, align_bytes=64)
+        hs = [hs_all[:, b * P : (b + 1) * P] for b in range(BLOCKS)]
+        ewg = [keep.tile([P, V // 2], U32, name="ewg0", align_bytes=64),
+               shared.tile([P, V // 2], U32, name="ewg1", offset=PICKED_ES_AT + 64, align_bytes=64)]
+        halves = [slice(0, V // 2), slice(V // 2, V)]
+        hb = []
         for b in range(BLOCKS):
-            cols = slice(b * P, (b + 1) * P)
             hp = psum.tile([P, PACK, P], F32, name=f"hp{b}", tag="acc", bufs=BLOCKS)
             for t in range(PACK):
                 tcols = slice(t * P, (t + 1) * P)
                 nc.tensor.matmul_mx(out=hp[:, t, :], lhsT=wc[:, tcols].bitcast(FP8X4), lhsT_scale=ws[:, tcols],
-                                    rhs=xwg[b].bitcast(FP8X4), rhs_scale=x_plane[:, cols], start=True, stop=True)
-            hb = keep.tile([P, P, PACK], BF16, name=f"hb{b}", align_bytes=64)
-            nc.scalar.copy(hb[:], hp[:].rearrange("p t n -> p n t"))
-            nc.vector.quantize_mx(out=hc[:, cols].bitcast(FP8X4), scales=hs[b], in_=hb[:].rearrange("p n t -> p (n t)"))
-            if b == 0:
-                nc.vector.tensor_copy(ewg[:], ew[:].indirect(pro_sb[:]))
+                                    rhs=xwg[b].bitcast(FP8X4), rhs_scale=x_plane[:, b * P : (b + 1) * P], start=True, stop=True)
+            hb.append(keep.tile([P, P, PACK], BF16, name=f"hb{b}", align_bytes=64))
+            nc.scalar.copy(hb[b][:], hp[:].rearrange("p t n -> p n t"))
+
+        def gather_e(half):
+            nc.vector.tensor_copy(ewg[half][:], ew[:].indirect(pro_sb[:, half * V // 32 : (half + 1) * V // 32]))
+
+        def quantise_h(b):
+            nc.vector.quantize_mx(out=hc[:, b * P : (b + 1) * P].bitcast(FP8X4), scales=hs[b], in_=hb[b][:].rearrange("p n t -> p (n t)"))
+
+        def product(b, half, dest):
+            nc.tensor.matmul_mx(out=dest, lhsT=hc[:, b * P : (b + 1) * P].bitcast(FP8X4), lhsT_scale=hs[b],
+                                rhs=ewg[half][:].bitcast(FP8X4), rhs_scale=e_plane[:, halves[half]], start=True, stop=True)
 
         z, neg_max, total, rest, base = {}, {}, {}, {}, {}
 
         def scale(b):
-            cols = slice(b * P, (b + 1) * P)
             yp = psum.tile([P, V], F32, name=f"yp{b}", tag="yp", bufs=2)
-            nc.tensor.matmul_mx(out=yp[:], lhsT=hc[:, cols].bitcast(FP8X4), lhsT_scale=hs[b],
-                                rhs=ewg[:].bitcast(FP8X4), rhs_scale=e_plane[:], start=True, stop=True)
+            for half in range(2):
+                product(b, half, yp[:, halves[half]])
             z[b] = keep.tile([P, V], F32, name=f"z{b}", align_bytes=64)
             nc.vector.tensor_tensor(z[b][:], yp[:], inv_all[:], ALU.mult)
 
@@ -185,7 +193,18 @@ def tile_picked_yphi_log_p_kernel(tc, x_words, x_scales, w1, e_words, e_scales, 
                 nc.vector.tensor_scalar(res[:, cols], z[b][:, cols], base[b][:], rest[b][:], ALU.add, ALU.add)
                 nc.sync.dma_start(out[b * P : (b + 1) * P, cols], res[:, cols])
 
-        scale(0)
+        gather_e(0)
+        quantise_h(0)
+        first = [psum.tile([P, V // 2], F32, name=f"first{half}", tag=bank) for half, bank in enumerate(("turned", "spread"))]
+        product(0, 0, first[0][:])
+        gather_e(1)
+        product(0, 1, first[1][:])
+        quantise_h(1)
+        quantise_h(2)
+        z[0] = keep.tile([P, V], F32, name="z0", align_bytes=64)
+        nc.vector.tensor_tensor(z[0][:, halves[0]], first[0][:], inv_all[:, halves[0]], ALU.mult)
+        quantise_h(3)
+        nc.vector.tensor_tensor(z[0][:, halves[1]], first[1][:], inv_all[:, halves[1]], ALU.mult)
         scale(1)
         row_max(0)
         row_sum(0)

@@ -27,7 +27,8 @@ LOG_ABOVE = 9
 NODES = LOG_BELOW + LOG_ABOVE + 1
 
 ROW0 = P - 16
-INV_SPLIT = 1536
+INV_SPLIT = 1280
+EARLY = 384
 X_PIECES = ((0, 1), (1, 2), (2, 4))
 W_BYTES = PACK * H * 4
 E_SCALES_AT = W_BYTES + 4 * W
@@ -52,8 +53,8 @@ def tile_picked_yphi_log_p_kernel(tc, x_words, x_scales, w1, e_words, e_scales, 
         xs = shared.tile([P, T], U8, name="xs", offset=W_BYTES, align_bytes=64)
         es = shared.tile([P, W], U8, name="es", offset=E_SCALES_AT, align_bytes=64)
         inv_row = keep.tile([P, W], F32, name="inv_row", align_bytes=64)
-        x_plane = keep.tile([P, S], U8, name="x_plane", align_bytes=64)
-        e_plane = keep.tile([P, V], U8, name="e_plane", align_bytes=64)
+        x_plane = keep.tile([P, EARLY], U8, name="x_plane", align_bytes=64)
+        late_plane = keep.tile([P, S - EARLY + V], U8, name="late_plane", align_bytes=64)
         steps = keep.tile([P, NODES], F32, name="steps")
         grid = keep.tile([P, NODES], F32, name="grid")
         nodes_up = keep.tile([P, NODES], F32, name="nodes_up")
@@ -68,7 +69,7 @@ def tile_picked_yphi_log_p_kernel(tc, x_words, x_scales, w1, e_words, e_scales, 
                 nc.sync.dma_start(plane[32 * q : 32 * q + 4, :].bitcast(I32), picked[ROW0 + 4 * q : ROW0 + 4 * q + 4, :].bitcast(I32))
 
         nc.sync.dma_start(offs_sb[:], offs)
-        nc.sync.dma_start(xs[ROW0:, :].bitcast(I32), x_scales[0].bitcast(I32))
+        nc.scalar.dma_start(xs[ROW0:, :].bitcast(I32), x_scales[0].bitcast(I32))
         nc.sync.dma_start(pro_sb[:], pro)
         nc.sync.dma_start(inv_row[P - 1 : P, :], inv[0:1, :])
         nc.sync.dma_start(es[ROW0:, :].bitcast(I32), e_scales[0].bitcast(I32))
@@ -86,16 +87,19 @@ def tile_picked_yphi_log_p_kernel(tc, x_words, x_scales, w1, e_words, e_scales, 
         nc.scalar.activation(nodes_up[:], steps[:], ACT.Exp, scale=LOG_STEP)
         nc.scalar.activation(inv_row[0 : P - 1, INV_SPLIT:], zero[0 : P - 1, :].to_broadcast([P - 1, W - INV_SPLIT]), ACT.Copy)
 
-        xsg = keep.tile([P, S], U8, name="xsg", align_bytes=64)
-        nc.vector.tensor_copy(xsg[:], xs[:].indirect(offs_sb[:]))
+        xsg = keep.tile([P, EARLY], U8, name="xsg", align_bytes=64)
+        late = shared.tile([P, S - EARLY + V], U8, name="late", offset=PICKED_ES_AT, align_bytes=64)
+        nc.vector.tensor_copy(xsg[:], xs[:].indirect(offs_sb[:, 0 : EARLY // 16]))
+        nc.vector.tensor_copy(late[:, 0 : S - EARLY], xs[:].indirect(offs_sb[:, EARLY // 16 :]))
         e_rows = e_words[0].rearrange("p n t -> p (n t)").bitcast(I32)
         place_scales(x_plane, xsg)
         nc.sync.dma_start(ew[:].bitcast(I32), e_rows)
         invg = keep.tile([P, V], F32, name="invg", align_bytes=64)
         nc.scalar.activation(invg[:], inv_row[:].indirect(pro_sb[:]), ACT.Copy)
-        esg = shared.tile([P, V], U8, name="esg", offset=PICKED_ES_AT, align_bytes=64)
-        nc.vector.tensor_copy(esg[:], es[:].indirect(pro_sb[:]))
-        place_scales(e_plane, esg)
+        nc.vector.tensor_copy(late[:, S - EARLY :], es[:].indirect(pro_sb[:]))
+        place_scales(late_plane, late)
+        x_planes = [x_plane[:, c : c + P] for c in range(0, EARLY, P)] + [late_plane[:, c : c + P] for c in range(0, S - EARLY, P)]
+        e_plane = late_plane[:, S - EARLY :]
 
         nc.scalar.mul(grid[:], nodes_up[:], -1.0)
 
@@ -147,7 +151,7 @@ def tile_picked_yphi_log_p_kernel(tc, x_words, x_scales, w1, e_words, e_scales, 
             for t in range(PACK):
                 tcols = slice(t * P, (t + 1) * P)
                 nc.tensor.matmul_mx(out=hp[:, t, :], lhsT=wc[:, tcols].bitcast(FP8X4), lhsT_scale=ws[:, tcols],
-                                    rhs=xwg[b].bitcast(FP8X4), rhs_scale=x_plane[:, b * P : (b + 1) * P], start=True, stop=True)
+                                    rhs=xwg[b].bitcast(FP8X4), rhs_scale=x_planes[b], start=True, stop=True)
             hb.append(keep.tile([P, P, PACK], BF16, name=f"hb{b}", align_bytes=64))
             nc.scalar.copy(hb[b][:], hp[:].rearrange("p t n -> p n t"))
 
@@ -199,12 +203,11 @@ def tile_picked_yphi_log_p_kernel(tc, x_words, x_scales, w1, e_words, e_scales, 
         product(0, 0, first[0][:])
         gather_e(1)
         product(0, 1, first[1][:])
-        quantise_h(1)
-        quantise_h(2)
         z[0] = keep.tile([P, V], F32, name="z0", align_bytes=64)
-        nc.vector.tensor_tensor(z[0][:, halves[0]], first[0][:], inv_all[:, halves[0]], ALU.mult)
+        for half in range(2):
+            quantise_h(half + 1)
+            nc.vector.tensor_tensor(z[0][:, halves[half]], first[half][:], inv_all[:, halves[half]], ALU.mult)
         quantise_h(3)
-        nc.vector.tensor_tensor(z[0][:, halves[1]], first[1][:], inv_all[:, halves[1]], ALU.mult)
         scale(1)
         row_max(0)
         row_sum(0)

@@ -27,7 +27,7 @@ LOG_ABOVE = 9
 NODES = LOG_BELOW + LOG_ABOVE + 1
 
 ROW0 = P - 16
-INV_SPLIT = 1280
+INV_SPLIT = 1536
 EARLY = 384
 X_PIECES = ((0, 1), (1, 2), (2, 4))
 W_BYTES = PACK * H * 4
@@ -137,7 +137,7 @@ def tile_picked_yphi_log_p_kernel(tc, x_words, x_scales, w1, e_words, e_scales, 
         for c in range(V // P):
             nc.tensor.transpose(spread[:, c * P : (c + 1) * P], inv_col[:, c : c + 1].to_broadcast([P, P]), ident[:])
         inv_all = keep.tile([P, V], F32, name="inv_all", align_bytes=64)
-        nc.scalar.copy(inv_all[:], spread[:])
+        nc.vector.tensor_copy(inv_all[:], spread[:])
 
         hc = keep.tile([P, S], U32, name="hc", align_bytes=64)
         hs_all = shared.tile([P, S], U8, name="hs_all", offset=PICKED_ES_AT + 64 - S, align_bytes=64)

@@ -78,9 +78,10 @@ def tile_picked_yphi_log_p_kernel(tc, x_words, x_scales, w1, e_words, e_scales, 
 
         zero = keep.tile([P, 1], F32, name="zero")
         nc.gpsimd.memset(zero[:], 0.0)
-        nc.gpsimd.memset(xs[0:ROW0, :].bitcast(I32), 0)
         nc.gpsimd.iota(steps[:], [[1, NODES]], base=-LOG_BELOW, channel_multiplier=0, allow_small_or_imprecise_dtypes=True)
-        make_identity(nc, ident[:])
+        nc.vector.memset(ident[:], 0.0)
+        make_identity(nc, ident[:], nomemset=True)
+        nc.vector.memset(xs[0:ROW0, :].bitcast(I32), 0)
         nc.vector.memset(inv_row[0 : P - 1, 0:INV_SPLIT], 0.0)
         nc.vector.memset(es[0:ROW0, :].bitcast(I32), 0)
 

@@ -27,7 +27,7 @@ LOG_ABOVE = 9
 NODES = LOG_BELOW + LOG_ABOVE + 1
 
 ROW0 = P - 16
-INV_SPLIT = 1536
+INV_SPLIT = 1920
 EARLY = 384
 X_PIECES = ((0, 1), (1, 2), (2, 4))
 W_BYTES = PACK * H * 4
@@ -72,7 +72,7 @@ def tile_picked_yphi_log_p_kernel(tc, x_words, x_scales, w1, e_words, e_scales, 
         nc.scalar.dma_start(xs[ROW0:, :].bitcast(I32), x_scales[0].bitcast(I32))
         nc.sync.dma_start(pro_sb[:], pro)
         nc.sync.dma_start(inv_row[P - 1 : P, :], inv[0:1, :])
-        nc.sync.dma_start(es[ROW0:, :].bitcast(I32), e_scales[0].bitcast(I32))
+        nc.scalar.dma_start(es[ROW0:, :].bitcast(I32), e_scales[0].bitcast(I32))
         nc.sync.dma_start(w_raw[:], w1.rearrange("(p j) c -> p j c", j=PACK))
         nc.sync.dma_start(xw[:].bitcast(I32), x_words[0].rearrange("p n t -> p (n t)").bitcast(I32))
 

import math
from contextlib import ExitStack

import concourse.mybir as mybir
from concourse.masks import make_identity

F32 = mybir.dt.float32
BF16 = mybir.dt.bfloat16
I32 = mybir.dt.int32
U32 = mybir.dt.uint32
U16 = mybir.dt.uint16
U8 = mybir.dt.uint8
FP8X4 = mybir.dt.float8_e4m3fn_x4
ACT = mybir.ActivationFunctionType
ALU = mybir.AluOpType
AXIS = mybir.AxisListType

P = 128
PACK = 4
QUADRANTS = 4
K, T, S, H, V, W = 512, 1024, 512, 512, 512, 2048
BLOCKS = S // P

LOG_STEP = 0.375
LOG_BELOW = 76
LOG_ABOVE = 9
NODES = LOG_BELOW + LOG_ABOVE + 1

ROW0 = P - 16
INV_SPLIT = 1920
EARLY = 384
X_PIECES = ((0, 1), (1, 2), (2, 4))
W_BYTES = PACK * H * 4
E_SCALES_AT = W_BYTES + 4 * W
PICKED_ES_AT = E_SCALES_AT + W + S

FLOPS = 2 * K * H * S + 2 * H * S * V
BYTES = K * T + K * T // 32 + 4 * K * H + H * W + H * W // 32 + 4 * W + 2 * P * (S + V) // 16 + 4 * S * V


def tile_picked_yphi_log_p_kernel(tc, x_words, x_scales, w1, e_words, e_scales, inv, offs, pro, out):
    nc = tc.nc
    sum_at_one = LOG_STEP * sum(math.e ** -(math.e ** (LOG_STEP * j)) for j in range(-LOG_BELOW, LOG_ABOVE + 1))
    log_of_step = math.log10(LOG_STEP) / math.log10(math.e)

    with ExitStack() as ctx:
        keep = ctx.enter_context(tc.tile_pool(name="keep", bufs=1))
        shared = ctx.enter_context(tc.tile_pool(name="shared", bufs=1))
        psum = ctx.enter_context(tc.psum_pool(name="psum", bufs=1))

        offs_sb = keep.tile([P, S // 16], U16, name="offs_sb")
        pro_sb = keep.tile([P, V // 16], U16, name="pro_sb")
        xs = shared.tile([P, T], U8, name="xs", offset=W_BYTES, align_bytes=64)
        es = shared.tile([P, W], U8, name="es", offset=E_SCALES_AT, align_bytes=64)
        inv_row = keep.tile([P, W], F32, name="inv_row", align_bytes=64)
        x_plane = keep.tile([P, EARLY], U8, name="x_plane", align_bytes=64)
        late_plane = keep.tile([P, S - EARLY + V], U8, name="late_plane", align_bytes=64)
        steps = keep.tile([P, NODES], F32, name="steps")
        grid = keep.tile([P, NODES], F32, name="grid")
        nodes_up = keep.tile([P, NODES], F32, name="nodes_up")
        ident = keep.tile([P, P], F32, name="ident", align_bytes=64)

        w_raw = shared.tile([P, PACK, H], F32, name="w_raw", offset=0, align_bytes=64)
        xw = keep.tile([P, T], U32, name="xw", align_bytes=64)
        ew = shared.tile([P, W], U32, name="ew", offset=W_BYTES, align_bytes=64)

        def place_scales(plane, picked):
            for q in range(QUADRANTS):
                nc.sync.dma_start(plane[32 * q : 32 * q + 4, :].bitcast(I32), picked[ROW0 + 4 * q : ROW0 + 4 * q + 4, :].bitcast(I32))

        nc.sync.dma_start(offs_sb[:], offs)
        nc.scalar.dma_start(xs[ROW0:, :].bitcast(I32), x_scales[0].bitcast(I32))
        nc.sync.dma_start(pro_sb[:], pro)
        nc.sync.dma_start(inv_row[P - 1 : P, :], inv[0:1, :])
        nc.scalar.dma_start(es[ROW0:, :].bitcast(I32), e_scales[0].bitcast(I32))
        nc.sync.dma_start(w_raw[:], w1.rearrange("(p j) c -> p j c", j=PACK))
        nc.sync.dma_start(xw[:].bitcast(I32), x_words[0].rearrange("p n t -> p (n t)").bitcast(I32))

        zero = keep.tile([P, 1], F32, name="zero")
        nc.gpsimd.memset(zero[:], 0.0)
        nc.gpsimd.iota(steps[:], [[1, NODES]], base=-LOG_BELOW, channel_multiplier=0, allow_small_or_imprecise_dtypes=True)
        nc.vector.memset(ident[:], 0.0)
        make_identity(nc, ident[:], nomemset=True)
        nc.vector.memset(xs[0:ROW0, :].bitcast(I32), 0)
        nc.vector.memset(inv_row[0 : P - 1, 0:INV_SPLIT], 0.0)
        nc.vector.memset(es[0:ROW0, :].bitcast(I32), 0)

        nc.scalar.activation(nodes_up[:], steps[:], ACT.Exp, scale=LOG_STEP)
        nc.scalar.activation(inv_row[0 : P - 1, INV_SPLIT:], zero[0 : P - 1, :].to_broadcast([P - 1, W - INV_SPLIT]), ACT.Copy)

        xsg = keep.tile([P, EARLY], U8, name="xsg", align_bytes=64)
        late = shared.tile([P, S - EARLY + V], U8, name="late", offset=PICKED_ES_AT, align_bytes=64)
        nc.vector.tensor_copy(xsg[:], xs[:].indirect(offs_sb[:, 0 : EARLY // 16]))
        nc.vector.tensor_copy(late[:, 0 : S - EARLY], xs[:].indirect(offs_sb[:, EARLY // 16 :]))
        e_rows = e_words[0].rearrange("p n t -> p (n t)").bitcast(I32)
        place_scales(x_plane, xsg)
        nc.sync.dma_start(ew[:].bitcast(I32), e_rows)
        invg = keep.tile([P, V], F32, name="invg", align_bytes=64)
        nc.scalar.activation(invg[:], inv_row[:].indirect(pro_sb[:]), ACT.Copy)
        nc.vector.tensor_copy(late[:, S - EARLY :], es[:].indirect(pro_sb[:]))
        place_scales(late_plane, late)
        x_planes = [x_plane[:, c : c + P] for c in range(0, EARLY, P)] + [late_plane[:, c : c + P] for c in range(0, S - EARLY, P)]
        e_plane = late_plane[:, S - EARLY :]

        nc.scalar.mul(grid[:], nodes_up[:], -1.0)

        wg = [keep.tile([P, 2, P, PACK], BF16, name=f"wg{pair}", align_bytes=64) for pair in range(2)]
        for pair, copy in enumerate((nc.vector.tensor_copy, nc.scalar.copy)):
            copy(wg[pair][:].rearrange("p t m j -> p m j t"),
                 w_raw[:].rearrange("p j (m t) -> p m j t", t=PACK)[:, :, :, 2 * pair : 2 * pair + 2])
        xwg = []

        def gather_x(b0, b1):
            if b0 == 0:
                piece = shared.tile([P, (b1 - b0) * P], U32, name="xwg0", offset=E_SCALES_AT, align_bytes=64)
            else:
                piece = shared.tile([P, (b1 - b0) * P], U32, name=f"xwg{b0}", offset=4 * P * b0, align_bytes=64)
            nc.vector.tensor_copy(piece[:], xw[:].indirect(offs_sb[:, b0 * P // 16 : b1 * P // 16]))
            xwg.extend(piece[:, (b - b0) * P : (b - b0 + 1) * P] for b in range(b0, b1))

        gather_x(*X_PIECES[0])
        wc = keep.tile([P, H], U32, name="wc", align_bytes=64)
        ws = keep.tile([P, H], U8, name="ws", align_bytes=64)
        for u in range(2):
            half = slice(u * H // 2, (u + 1) * H // 2)
            nc.vector.quantize_mx(out=wc[:, half].bitcast(FP8X4), scales=ws[:, half],
                                  in_=wg[u][:].rearrange("p t m j -> p (t m j)"))

        for piece in X_PIECES[1:]:
            gather_x(*piece)

        turned = psum.tile([P, V // P, P], F32, name="turned", tag="turned")
        for c in range(V // P):
            nc.tensor.transpose(turned[:, c, :], invg[:, c * P : (c + 1) * P], ident[:])
        inv_col = shared.tile([P, V // P], F32, name="inv_col", offset=E_SCALES_AT + 4 * P, align_bytes=64)
        nc.vector.tensor_copy(inv_col[:], turned[:, :, P - 1])
        spread = psum.tile([P, V], F32, name="spread", tag="spread")
        for c in range(V // P):
            nc.tensor.transpose(spread[:, c * P : (c + 1) * P], inv_col[:, c : c + 1].to_broadcast([P, P]), ident[:])
        inv_all = keep.tile([P, V], F32, name="inv_all", align_bytes=64)
        nc.vector.tensor_copy(inv_all[:], spread[:])

        hc = keep.tile([P, S], U32, name="hc", align_bytes=64)
        hs_all = shared.tile([P, S], U8, name="hs_all", offset=PICKED_ES_AT + 64 - S, align_bytes=64)
        hs = [hs_all[:, b * P : (b + 1) * P] for b in range(BLOCKS)]
        ewg = [keep.tile([P, V // 2], U32, name="ewg0", align_bytes=64),
               shared.tile([P, V // 2], U32, name="ewg1", offset=PICKED_ES_AT + 64, align_bytes=64)]
        halves = [slice(0, V // 2), slice(V // 2, V)]
        hb = []
        for b in range(BLOCKS):
            hp = psum.tile([P, PACK, P], F32, name=f"hp{b}", tag="acc", bufs=BLOCKS)
            for t in range(PACK):
                tcols = slice(t * P, (t + 1) * P)
                nc.tensor.matmul_mx(out=hp[:, t, :], lhsT=wc[:, tcols].bitcast(FP8X4), lhsT_scale=ws[:, tcols],
                                    rhs=xwg[b].bitcast(FP8X4), rhs_scale=x_planes[b], start=True, stop=True)
            hb.append(keep.tile([P, P, PACK], BF16, name=f"hb{b}", align_bytes=64))
            nc.scalar.copy(hb[b][:], hp[:].rearrange("p t n -> p n t"))

        def gather_e(half):
            nc.vector.tensor_copy(ewg[half][:], ew[:].indirect(pro_sb[:, half * V // 32 : (half + 1) * V // 32]))

        def quantise_h(b):
            nc.vector.quantize_mx(out=hc[:, b * P : (b + 1) * P].bitcast(FP8X4), scales=hs[b], in_=hb[b][:].rearrange("p n t -> p (n t)"))

        def product(b, half, dest):
            nc.tensor.matmul_mx(out=dest, lhsT=hc[:, b * P : (b + 1) * P].bitcast(FP8X4), lhsT_scale=hs[b],
                                rhs=ewg[half][:].bitcast(FP8X4), rhs_scale=e_plane[:, halves[half]], start=True, stop=True)

        z, neg_max, total, rest, base = {}, {}, {}, {}, {}

        def scale(b):
            yp = psum.tile([P, V], F32, name=f"yp{b}", tag="yp", bufs=2)
            for half in range(2):
                product(b, half, yp[:, halves[half]])
            z[b] = keep.tile([P, V], F32, name=f"z{b}", align_bytes=64)
            nc.vector.tensor_tensor(z[b][:], yp[:], inv_all[:], ALU.mult)

        def row_max(b):
            neg_max[b] = keep.tile([P, 1], F32, name=f"neg_max{b}")
            nc.vector.tensor_reduce(neg_max[b][:], z[b][:], AXIS.X, ALU.max, negate=True)

        def row_sum(b):
            total[b] = keep.tile([P, 1], F32, name=f"total{b}")
            terms = keep.tile([P, V], F32, name=f"terms{b}", align_bytes=64)
            nc.scalar.activation(terms[:], z[b][:], ACT.Exp, bias=neg_max[b][:], accum_out=total[b][:])
            base[b] = keep.tile([P, 1], F32, name=f"base{b}")
            nc.scalar.activation(base[b][:], neg_max[b][:], ACT.Identity, bias=-sum_at_one)

        def row_log(b):
            rest[b] = keep.tile([P, 1], F32, name=f"rest{b}")
            terms = keep.tile([P, NODES], F32, name=f"log_terms{b}", align_bytes=64)
            nc.scalar.activation(terms[:], grid[:], ACT.Exp, bias=log_of_step, scale=total[b][:], accum_out=rest[b][:])

        def finish(b, pieces):
            res = keep.tile([P, V], F32, name=f"res{b}", align_bytes=64)
            for c0 in range(0, V, V // pieces):
                cols = slice(c0, c0 + V // pieces)
                nc.vector.tensor_scalar(res[:, cols], z[b][:, cols], base[b][:], rest[b][:], ALU.add, ALU.add)
                nc.sync.dma_start(out[b * P : (b + 1) * P, cols], res[:, cols])

        gather_e(0)
        quantise_h(0)
        first = [psum.tile([P, V // 2], F32, name=f"first{half}", tag=bank) for half, bank in enumerate(("turned", "spread"))]
        product(0, 0, first[0][:])
        gather_e(1)
        product(0, 1, first[1][:])
        z[0] = keep.tile([P, V], F32, name="z0", align_bytes=64)
        for half in range(2):
            quantise_h(half + 1)
            nc.vector.tensor_tensor(z[0][:, halves[half]], first[half][:], inv_all[:, halves[half]], ALU.mult)
        quantise_h(3)
        scale(1)
        row_max(0)
        row_sum(0)
        row_log(0)
        scale(2)
        row_max(1)
        row_sum(1)
        row_max(2)
        row_sum(2)
        row_log(1)
        row_log(2)
        scale(3)
        finish(0, 1)
        row_max(3)
        row_sum(3)
        row_log(3)
        finish(1, 1)
        finish(2, 1)
        finish(3, 2)
